import numpy as np
import ml_dtypes


def mxq(x, axis, fmt="e4m3"):
    dtype, down = {"e4m3": (ml_dtypes.float8_e4m3fn, 7), "e5m2": (ml_dtypes.float8_e5m2, 14)}[fmt]
    v = np.moveaxis(np.asarray(x, np.float32).astype(ml_dtypes.bfloat16).astype(np.float64), axis, -1)
    blocks = v.reshape(v.shape[:-1] + (-1, 32))
    amax = np.abs(blocks).max(-1, keepdims=True)
    byte = np.maximum(np.where(amax > 0, np.frexp(amax)[1] - 1 + 127, 0) - down, 1)
    scale = np.exp2(byte - 127.0)
    codes = (blocks / scale).astype(np.float32).astype(dtype).astype(np.float64)
    return np.moveaxis((codes * scale).reshape(v.shape), -1, axis)


WIDE = False


def mx_kscale(k):
    if not WIDE:
        return np.ones(k)
    levels = np.array([10, -10, 5, -5, 0])
    if k % 512:
        return np.exp2(np.random.permutation(np.resize(levels, k // 32))).repeat(32)
    a = np.empty((k // 512, 16))
    for p in range(k // 512):
        a[p, :8] = np.random.permutation(np.resize(levels, 8))
        for g in range(8):
            far = levels[np.abs(levels - a[p, g]) >= 10]
            a[p, g + 8] = far[np.random.randint(len(far))]
    return np.exp2(a.ravel()).repeat(32)


def f64(x):
    return np.asarray(x).astype(np.float64)


def striped(idx):
    return np.tile(idx.reshape(-1, 16).T, (8, 1)).astype(np.uint16)


def unstriped(offs):
    return offs[:16].T.reshape(-1).astype(np.int64)


def relu(v):
    return np.maximum(v, 0.0)


K, T, D, S, V, N = 512, 2048, 3, 1536, 512, 512


def setup_inputs():
    n = np.random.standard_normal
    s = mx_kscale(K)[:, None]
    return {
        "xT": (n((K, T)) * s / np.sqrt(D)).astype(ml_dtypes.bfloat16).astype(np.float32),
        "w": (n((K, N)) / np.sqrt(K) / s).astype(np.float32),
        "b": (0.3 * n((N, 1))).astype(np.float32),
        "offs": striped(np.concatenate([np.random.permutation(T)[:V] for _ in range(D)])),
    }


def reference(xT, w, b, offs):
    idx = unstriped(offs)
    x = sum(f64(xT)[:, idx[d * V:(d + 1) * V]] for d in range(D))
    return relu((mxq(f64(w), 0, "e4m3").T @ mxq(x, 0, "e4m3")) + f64(b))

@@ -1,0 +1,157 @@
+from contextlib import ExitStack
+
+import concourse.mybir as mybir
+
+K, T, D, V, N = 512, 2048, 3, 512, 512
+FLOPS = 2 * K * N * V
+
+F32 = mybir.dt.float32
+BF16 = mybir.dt.bfloat16
+U32 = mybir.dt.uint32
+U16 = mybir.dt.uint16
+U8 = mybir.dt.uint8
+FP8X4 = mybir.dt.float8_e4m3fn_x4
+ADD = mybir.AluOpType.add
+MAX = mybir.AluOpType.max
+RELU = mybir.ActivationFunctionType.Relu
+
+P = 128
+PACK = 4
+PAIRS = 2
+CHUNK = 512
+HALF = V // 2
+M_TILES = N // P
+
+
+def tile_picked_hash_lin_relu_sub_l_kernel(tc, xT, w, b, offs, out):
+    nc = tc.nc
+    with ExitStack() as ctx:
+        keep = ctx.enter_context(tc.tile_pool(name="keep", bufs=1))
+        psum = ctx.enter_context(tc.psum_pool(name="psum", bufs=1))
+
+        offsets = keep.tile([P, D * V // 16], U16, name="offsets")
+        bias = keep.tile([P, M_TILES], F32, name="bias")
+        warm = keep.tile([P, 8], F32, name="warm")
+        warm_out = keep.tile([P, 8], F32, name="warm_out")
+        nc.vector.memset(warm[:], 0.0)
+        nc.scalar.activation(warm_out[:], warm[:], RELU)
+
+        x_rows = xT.rearrange("(p t) c -> p t c", t=PACK)
+        n_chunks = T // CHUNK
+        raw = {}
+        for u in range(PAIRS):
+            for c in range(n_chunks):
+                raw[u, c] = keep.tile([P, 2, CHUNK], F32, name="raw%d_%d" % (u, c))
+                nc.sync.dma_start(out=raw[u, c][:], in_=x_rows[:, 2 * u : 2 * u + 2, c * CHUNK : (c + 1) * CHUNK])
+            if u == 0:
+                nc.sync.dma_start(offsets[:], offs)
+        w_raw = keep.tile([P, PACK, N], F32, name="w_raw")
+        nc.sync.dma_start(out=w_raw[:], in_=w.rearrange("(p t) m -> p t m", t=PACK))
+        with nc.allow_non_contiguous_dma(reason="one bias value a partition"):
+            nc.sync.dma_start(out=bias[:], in_=b.rearrange("(j p) o -> p (j o)", p=P))
+
+        tables = [keep.tile([P, 2 * T], BF16, name="table%d" % u, align_bytes=64) for u in range(PAIRS)]
+
+        def cast(engine, u, c, lo, hi):
+            dst = tables[u][:].rearrange("p (c e) -> p c e", e=2)[:, c * CHUNK + lo : c * CHUNK + hi, :]
+            src = raw[u, c][:, :, lo:hi].rearrange("p e c -> p c e")
+            if engine == "vector":
+                nc.vector.tensor_copy(out=dst, in_=src)
+            else:
+                nc.scalar.copy(out=dst, in_=src)
+
+        HW = 2 * HALF
+        first = [keep.tile([P, 2, 2 * V], BF16, name="first%d" % u, align_bytes=64) for u in range(PAIRS)]
+        shared = keep.tile([P, 3 * HW + N * PACK], BF16, name="shared", align_bytes=64)
+        w_bf = shared[:, 3 * HW :]
+        partial = keep.tile([P, PAIRS, 2 * V], F32, name="partial", align_bytes=64)
+
+        def look_up(dst, u, start, count):
+            window = tables[u][:].bitcast(U32).indirect(offsets[:, start // 16 : (start + count) // 16])
+            nc.vector.tensor_copy(out=dst.bitcast(U32), in_=window)
+
+        def gather(u, d, h):
+            if d < 2:
+                dst = first[u][:, d, h * HW : (h + 1) * HW]
+            else:
+                dst = shared[:, (2 * h + u) * HW : (2 * h + u + 1) * HW]
+            look_up(dst, u, d * V + h * HALF, HALF)
+
+        def add_first(u, h):
+            cols = slice(h * HW, (h + 1) * HW)
+            nc.vector.tensor_tensor(partial[:, u, cols], first[u][:, 0, cols], first[u][:, 1, cols], ADD)
+
+        x_bf = [keep.tile([P, HALF * PACK], BF16, name="x_bf%d" % h, align_bytes=64) for h in range(2)]
+        x_codes = [keep.tile([P, HALF], U32, name="x_codes%d" % h, align_bytes=64) for h in range(2)]
+        x_scales = [keep.tile([P, HALF], U8, name="x_scales%d" % h, align_bytes=64) for h in range(2)]
+        w_codes = keep.tile([P, N], U32, name="w_codes", align_bytes=64)
+        w_scales = keep.tile([P, N], U8, name="w_scales", align_bytes=64)
+
+        def add_last(h):
+            nc.vector.tensor_tensor(
+                x_bf[h][:].rearrange("p (v u e) -> p v u e", u=PAIRS, e=2),
+                partial[:, :, h * HW : (h + 1) * HW].rearrange("p u (v e) -> p v u e", e=2),
+                shared[:, 2 * h * HW : (2 * h + 2) * HW].rearrange("p (u v e) -> p v u e", u=PAIRS, e=2),
+                ADD,
+            )
+
+        def quantize_x(h):
+            nc.vector.quantize_mx(out=x_codes[h][:].bitcast(FP8X4), scales=x_scales[h][:], in_=x_bf[h][:])
+
+        out_rows = out.rearrange("(j p) v -> p j v", p=P)
+
+        def product(h):
+            cols = slice(h * HALF, (h + 1) * HALF)
+            result = keep.tile([P, M_TILES, HALF], F32, name="result%d" % h)
+            for j in range(M_TILES):
+                acc = psum.tile([P, HALF], F32, name="acc%d_%d" % (h, j))
+                m_cols = slice(j * P, (j + 1) * P)
+                nc.tensor.matmul_mx(
+                    out=acc[:],
+                    lhsT=w_codes[:, m_cols].bitcast(FP8X4),
+                    lhsT_scale=w_scales[:, m_cols],
+                    rhs=x_codes[h][:].bitcast(FP8X4),
+                    rhs_scale=x_scales[h][:],
+                    start=True,
+                    stop=True,
+                )
+                if h == 1 and j % 2 == 1:
+                    nc.vector.tensor_scalar(result[:, j, :], acc[:], bias[:, j : j + 1], 0.0, ADD, MAX)
+                else:
+                    nc.scalar.activation(result[:, j, :], acc[:], RELU, bias=bias[:, j : j + 1])
+                if j % 2 == 1:
+                    nc.sync.dma_start(out=out_rows[:, j - 1 : j + 1, cols], in_=result[:, j - 1 : j + 1, :])
+
+        SPLIT = 352
+        for c in range(n_chunks - 1):
+            cast("vector", 0, c, 0, CHUNK)
+        cast("vector", 0, n_chunks - 1, 0, SPLIT)
+        cast("scalar", 0, n_chunks - 1, SPLIT, CHUNK)
+        for c in range(n_chunks - 1):
+            cast("scalar", 1, c, 0, CHUNK)
+        cast("scalar", 1, n_chunks - 1, SPLIT, CHUNK)
+        look_up(first[0][:].rearrange("p d c -> p (d c)"), 0, 0, 2 * V)
+        gather(0, 2, 0)
+        gather(0, 2, 1)
+        add_first(0, 0)
+        cast("vector", 1, n_chunks - 1, 0, SPLIT)
+        nc.scalar.copy(
+            out=w_bf.rearrange("p (c i t) -> p c t i", i=4, t=PACK),
+            in_=w_raw[:].rearrange("p t (c i) -> p c t i", i=4),
+        )
+        add_first(0, 1)
+        gather(1, 0, 0)
+        gather(1, 1, 0)
+        gather(1, 2, 0)
+        add_first(1, 0)
+        gather(1, 0, 1)
+        add_last(0)
+        gather(1, 1, 1)
+        quantize_x(0)
+        nc.vector.quantize_mx(out=w_codes[:].bitcast(FP8X4), scales=w_scales[:], in_=w_bf)
+        add_first(1, 1)
+        product(0)
+        gather(1, 2, 1)
+        add_last(1)
+        quantize_x(1)
+        product(1)

@@ -14,13 +14,18 @@ FP8X4 = mybir.dt.float8_e4m3fn_x4
 ADD = mybir.AluOpType.add
 MAX = mybir.AluOpType.max
 RELU = mybir.ActivationFunctionType.Relu
+COPY = mybir.ActivationFunctionType.Copy
 
 P = 128
 PACK = 4
-PAIRS = 2
-CHUNK = 512
 HALF = V // 2
+HW = 2 * HALF
+QUARTER = V // 4
 M_TILES = N // P
+EARLY_CUTS = (0, 1024, 2048)
+PAIR_CUTS = (0, 1024, 1536, 2048)
+SCALAR_SHARE = 144
+LATE_CUTS = (0, 512, 1024, 1536, 2048)
 
 
 def tile_picked_hash_lin_relu_sub_l_kernel(tc, xT, w, b, offs, out):
@@ -37,121 +42,146 @@ def tile_picked_hash_lin_relu_sub_l_kernel(tc, xT, w, b, offs, out):
         nc.scalar.activation(warm_out[:], warm[:], RELU)
 
         x_rows = xT.rearrange("(p t) c -> p t c", t=PACK)
-        n_chunks = T // CHUNK
-        raw = {}
-        for u in range(PAIRS):
-            for c in range(n_chunks):
-                raw[u, c] = keep.tile([P, 2, CHUNK], F32, name="raw%d_%d" % (u, c))
-                nc.sync.dma_start(out=raw[u, c][:], in_=x_rows[:, 2 * u : 2 * u + 2, c * CHUNK : (c + 1) * CHUNK])
-            if u == 0:
-                nc.sync.dma_start(offsets[:], offs)
+
+        def load(name, t0, t1, cuts):
+            pieces = []
+            for lo, hi in zip(cuts, cuts[1:]):
+                piece = keep.tile([P, t1 - t0, hi - lo], F32, name="%s%d" % (name, lo))
+                nc.sync.dma_start(out=piece[:], in_=x_rows[:, t0:t1, lo:hi])
+                pieces.append((piece, lo, hi))
+            return pieces
+
+        early_raw = load("early", 0, 1, EARLY_CUTS)
+        nc.sync.dma_start(offsets[:], offs)
+        pair_raw = load("pair", 2, 4, PAIR_CUTS)
+        late_raw = load("late", 1, 2, LATE_CUTS)
         w_raw = keep.tile([P, PACK, N], F32, name="w_raw")
         nc.sync.dma_start(out=w_raw[:], in_=w.rearrange("(p t) m -> p t m", t=PACK))
         with nc.allow_non_contiguous_dma(reason="one bias value a partition"):
             nc.sync.dma_start(out=bias[:], in_=b.rearrange("(j p) o -> p (j o)", p=P))
 
-        tables = [keep.tile([P, 2 * T], BF16, name="table%d" % u, align_bytes=64) for u in range(PAIRS)]
-
-        def cast(engine, u, c, lo, hi):
-            dst = tables[u][:].rearrange("p (c e) -> p c e", e=2)[:, c * CHUNK + lo : c * CHUNK + hi, :]
-            src = raw[u, c][:, :, lo:hi].rearrange("p e c -> p c e")
-            if engine == "vector":
-                nc.vector.tensor_copy(out=dst, in_=src)
-            else:
-                nc.scalar.copy(out=dst, in_=src)
-
-        HW = 2 * HALF
-        first = [keep.tile([P, 2, 2 * V], BF16, name="first%d" % u, align_bytes=64) for u in range(PAIRS)]
-        shared = keep.tile([P, 3 * HW + N * PACK], BF16, name="shared", align_bytes=64)
-        w_bf = shared[:, 3 * HW :]
-        partial = keep.tile([P, PAIRS, 2 * V], F32, name="partial", align_bytes=64)
-
-        def look_up(dst, u, start, count):
-            window = tables[u][:].bitcast(U32).indirect(offsets[:, start // 16 : (start + count) // 16])
-            nc.vector.tensor_copy(out=dst.bitcast(U32), in_=window)
-
-        def gather(u, d, h):
-            if d < 2:
-                dst = first[u][:, d, h * HW : (h + 1) * HW]
-            else:
-                dst = shared[:, (2 * h + u) * HW : (2 * h + u + 1) * HW]
-            look_up(dst, u, d * V + h * HALF, HALF)
-
-        def add_first(u, h):
-            cols = slice(h * HW, (h + 1) * HW)
-            nc.vector.tensor_tensor(partial[:, u, cols], first[u][:, 0, cols], first[u][:, 1, cols], ADD)
-
-        x_bf = [keep.tile([P, HALF * PACK], BF16, name="x_bf%d" % h, align_bytes=64) for h in range(2)]
-        x_codes = [keep.tile([P, HALF], U32, name="x_codes%d" % h, align_bytes=64) for h in range(2)]
-        x_scales = [keep.tile([P, HALF], U8, name="x_scales%d" % h, align_bytes=64) for h in range(2)]
+        singles = [keep.tile([P, T], BF16, name="single%d" % e, align_bytes=64) for e in range(2)]
+        pairs = keep.tile([P, 2 * T], BF16, name="pairs", align_bytes=64)
+        picked = keep.tile([P, D, 2, 2 * V], BF16, name="picked", align_bytes=64)
+        partial = keep.tile([P, 2, 2 * V], F32, name="partial", align_bytes=64)
+        w_bf = keep.tile([P, N * PACK], BF16, name="w_bf", align_bytes=64)
+        x_bf0 = keep.tile([P, HALF * PACK], BF16, name="x_bf0", align_bytes=64)
+        x_bf = [x_bf0[:], w_bf[:, HALF * PACK :]]
+        x_codes = keep.tile([P, V], U32, name="x_codes", align_bytes=64)
+        x_scales = keep.tile([P, V], U8, name="x_scales", align_bytes=64)
         w_codes = keep.tile([P, N], U32, name="w_codes", align_bytes=64)
         w_scales = keep.tile([P, N], U8, name="w_scales", align_bytes=64)
 
-        def add_last(h):
+        def entries(d, v0, v1):
+            return offsets[:, (d * V + v0) // 16 : (d * V + v1) // 16]
+
+        def gather_single(e, d, v0, v1):
+            dst = picked[:, d, 0, 2 * v0 : 2 * v1].rearrange("p (v e) -> p v e", e=2)[:, :, e]
+            nc.scalar.activation(dst, singles[e][:].indirect(entries(d, v0, v1)), COPY)
+
+        def gather_pair(d, v0, v1):
+            window = pairs[:].bitcast(U32).indirect(entries(d, v0, v1))
+            nc.vector.tensor_copy(out=picked[:, d, 1, 2 * v0 : 2 * v1].bitcast(U32), in_=window)
+
+        def add_first(engine, u, v0, v1):
+            cols = slice(2 * v0, 2 * v1)
+            engine.tensor_tensor(partial[:, u, cols], picked[:, 0, u, cols], picked[:, 1, u, cols], ADD)
+
+        def summed(v0, v1):
+            h = v0 // HALF
+            return x_bf[h][:, PACK * (v0 - h * HALF) : PACK * (v1 - h * HALF)]
+
+        def add_last(v0, v1):
+            cols = slice(2 * v0, 2 * v1)
             nc.vector.tensor_tensor(
-                x_bf[h][:].rearrange("p (v u e) -> p v u e", u=PAIRS, e=2),
-                partial[:, :, h * HW : (h + 1) * HW].rearrange("p u (v e) -> p v u e", e=2),
-                shared[:, 2 * h * HW : (2 * h + 2) * HW].rearrange("p (u v e) -> p v u e", u=PAIRS, e=2),
+                summed(v0, v1).rearrange("p (v u e) -> p v u e", u=2, e=2),
+                partial[:, :, cols].rearrange("p u (v e) -> p v u e", e=2),
+                picked[:, 2, :, cols].rearrange("p u (v e) -> p v u e", e=2),
                 ADD,
             )
 
-        def quantize_x(h):
-            nc.vector.quantize_mx(out=x_codes[h][:].bitcast(FP8X4), scales=x_scales[h][:], in_=x_bf[h][:])
+        def quantize_x(v0, v1):
+            nc.vector.quantize_mx(out=x_codes[:, v0:v1].bitcast(FP8X4), scales=x_scales[:, v0:v1], in_=summed(v0, v1))
+
+        def cast_w(copy, s):
+            m0, m1 = s * N // 2, (s + 1) * N // 2
+            copy(
+                out=w_bf[:, PACK * m0 : PACK * m1].rearrange("p (c i t) -> p c t i", i=4, t=PACK),
+                in_=w_raw[:, :, m0:m1].rearrange("p t (c i) -> p c t i", i=4),
+            )
+
+        def quantize_w(s):
+            m0, m1 = s * N // 2, (s + 1) * N // 2
+            nc.vector.quantize_mx(
+                out=w_codes[:, m0:m1].bitcast(FP8X4), scales=w_scales[:, m0:m1], in_=w_bf[:, PACK * m0 : PACK * m1]
+            )
 
         out_rows = out.rearrange("(j p) v -> p j v", p=P)
 
-        def product(h):
-            cols = slice(h * HALF, (h + 1) * HALF)
-            result = keep.tile([P, M_TILES, HALF], F32, name="result%d" % h)
-            for j in range(M_TILES):
-                acc = psum.tile([P, HALF], F32, name="acc%d_%d" % (h, j))
-                m_cols = slice(j * P, (j + 1) * P)
-                nc.tensor.matmul_mx(
-                    out=acc[:],
-                    lhsT=w_codes[:, m_cols].bitcast(FP8X4),
-                    lhsT_scale=w_scales[:, m_cols],
-                    rhs=x_codes[h][:].bitcast(FP8X4),
-                    rhs_scale=x_scales[h][:],
-                    start=True,
-                    stop=True,
-                )
-                if h == 1 and j % 2 == 1:
-                    nc.vector.tensor_scalar(result[:, j, :], acc[:], bias[:, j : j + 1], 0.0, ADD, MAX)
-                else:
-                    nc.scalar.activation(result[:, j, :], acc[:], RELU, bias=bias[:, j : j + 1])
-                if j % 2 == 1:
-                    nc.sync.dma_start(out=out_rows[:, j - 1 : j + 1, cols], in_=result[:, j - 1 : j + 1, :])
+        def multiply(acc, j, v0, v1):
+            m_cols = slice(j * P, (j + 1) * P)
+            nc.tensor.matmul_mx(
+                out=acc,
+                lhsT=w_codes[:, m_cols].bitcast(FP8X4),
+                lhsT_scale=w_scales[:, m_cols],
+                rhs=x_codes[:, v0:v1].bitcast(FP8X4),
+                rhs_scale=x_scales[:, v0:v1],
+                start=True,
+                stop=True,
+            )
 
-        SPLIT = 352
-        for c in range(n_chunks - 1):
-            cast("vector", 0, c, 0, CHUNK)
-        cast("vector", 0, n_chunks - 1, 0, SPLIT)
-        cast("scalar", 0, n_chunks - 1, SPLIT, CHUNK)
-        for c in range(n_chunks - 1):
-            cast("scalar", 1, c, 0, CHUNK)
-        cast("scalar", 1, n_chunks - 1, SPLIT, CHUNK)
-        look_up(first[0][:].rearrange("p d c -> p (d c)"), 0, 0, 2 * V)
-        gather(0, 2, 0)
-        gather(0, 2, 1)
-        add_first(0, 0)
-        cast("vector", 1, n_chunks - 1, 0, SPLIT)
-        nc.scalar.copy(
-            out=w_bf.rearrange("p (c i t) -> p c t i", i=4, t=PACK),
-            in_=w_raw[:].rearrange("p t (c i) -> p c t i", i=4),
-        )
-        add_first(0, 1)
-        gather(1, 0, 0)
-        gather(1, 1, 0)
-        gather(1, 2, 0)
-        add_first(1, 0)
-        gather(1, 0, 1)
-        add_last(0)
-        gather(1, 1, 1)
-        quantize_x(0)
-        nc.vector.quantize_mx(out=w_codes[:].bitcast(FP8X4), scales=w_scales[:], in_=w_bf)
-        add_first(1, 1)
-        product(0)
-        gather(1, 2, 1)
-        add_last(1)
-        quantize_x(1)
-        product(1)
+        def product(v0, v1, per_bank, on_vector, per_store):
+            result = keep.tile([P, M_TILES, v1 - v0], F32, name="result%d" % v0)
+            for j0 in range(0, M_TILES, per_bank):
+                acc = psum.tile([P, per_bank, v1 - v0], F32, name="acc%d_%d" % (v0, j0))
+                for i in range(per_bank):
+                    multiply(acc[:, i, :], j0 + i, v0, v1)
+                for i in range(per_bank):
+                    j = j0 + i
+                    if j in on_vector:
+                        nc.vector.tensor_scalar(result[:, j, :], acc[:, i, :], bias[:, j : j + 1], 0.0, ADD, MAX)
+                    else:
+                        nc.scalar.activation(result[:, j, :], acc[:, i, :], RELU, bias=bias[:, j : j + 1])
+                    if (j + 1) % per_store == 0:
+                        rows = slice(j + 1 - per_store, j + 1)
+                        nc.sync.dma_start(out=out_rows[:, rows, v0:v1], in_=result[:, rows, :])
+
+        for piece, lo, hi in early_raw:
+            nc.vector.tensor_copy(out=singles[0][:, lo:hi], in_=piece[:, 0, :])
+        for d in range(D):
+            gather_single(0, d, 0, V)
+        def cast_pair(copy, piece, lo, c0, c1):
+            copy(
+                out=pairs[:, 2 * c0 : 2 * c1].rearrange("p (c e) -> p c e", e=2),
+                in_=piece[:, :, c0 - lo : c1 - lo].rearrange("p e c -> p c e"),
+            )
+
+        for piece, lo, hi in pair_raw:
+            cast_pair(nc.vector.tensor_copy, piece, lo, lo, min(hi, T - SCALAR_SHARE))
+            if hi == T:
+                cast_pair(nc.scalar.copy, piece, lo, T - SCALAR_SHARE, T)
+        for piece, lo, hi in late_raw:
+            nc.scalar.copy(out=singles[1][:, lo:hi], in_=piece[:, 0, :])
+        for h in range(2):
+            gather_pair(0, h * HALF, (h + 1) * HALF)
+            gather_pair(1, h * HALF, (h + 1) * HALF)
+            add_first(nc.gpsimd, 1, h * HALF, (h + 1) * HALF)
+        gather_pair(2, 0, V)
+        for h in range(2):
+            for d in range(D):
+                gather_single(1, d, h * HALF, (h + 1) * HALF)
+        add_first(nc.vector, 0, 0, HALF)
+        cast_w(nc.vector.tensor_copy, 0)
+        cast_w(nc.scalar.copy, 1)
+        add_last(0, HALF)
+        quantize_w(0)
+        quantize_x(0, HALF)
+        add_first(nc.vector, 0, HALF, V)
+        quantize_w(1)
+        product(0, HALF, 2, (), 2)
+        add_last(HALF, HALF + QUARTER)
+        add_last(HALF + QUARTER, V)
+        quantize_x(HALF, HALF + QUARTER)
+        quantize_x(HALF + QUARTER, V)
+        product(HALF, HALF + QUARTER, 2, (2, 3), 4)
+        product(HALF + QUARTER, V, 1, (1, 3), 4)

@@ -19,13 +19,11 @@ COPY = mybir.ActivationFunctionType.Copy
 P = 128
 PACK = 4
 HALF = V // 2
-HW = 2 * HALF
 QUARTER = V // 4
 M_TILES = N // P
-EARLY_CUTS = (0, 1024, 2048)
-PAIR_CUTS = (0, 1024, 1536, 2048)
-SCALAR_SHARE = 144
-LATE_CUTS = (0, 512, 1024, 1536, 2048)
+FIRST_CUT = 1536
+PAIR_CUTS = (0, 1152, 1728, 2048)
+LAST_CUTS = (0, 512, 1024, 1536, 2048)
 
 
 def tile_picked_hash_lin_relu_sub_l_kernel(tc, xT, w, b, offs, out):
@@ -42,146 +40,155 @@ def tile_picked_hash_lin_relu_sub_l_kernel(tc, xT, w, b, offs, out):
         nc.scalar.activation(warm_out[:], warm[:], RELU)
 
         x_rows = xT.rearrange("(p t) c -> p t c", t=PACK)
-
-        def load(name, t0, t1, cuts):
-            pieces = []
-            for lo, hi in zip(cuts, cuts[1:]):
-                piece = keep.tile([P, t1 - t0, hi - lo], F32, name="%s%d" % (name, lo))
-                nc.sync.dma_start(out=piece[:], in_=x_rows[:, t0:t1, lo:hi])
-                pieces.append((piece, lo, hi))
-            return pieces
-
-        early_raw = load("early", 0, 1, EARLY_CUTS)
+        rows = [keep.tile([P, T], F32, name="row%d" % e) for e in range(2)]
+        nc.sync.dma_start(out=rows[0][:, :FIRST_CUT], in_=x_rows[:, 2, :FIRST_CUT])
         nc.sync.dma_start(offsets[:], offs)
-        pair_raw = load("pair", 2, 4, PAIR_CUTS)
-        late_raw = load("late", 1, 2, LATE_CUTS)
-        w_raw = keep.tile([P, PACK, N], F32, name="w_raw")
-        nc.sync.dma_start(out=w_raw[:], in_=w.rearrange("(p t) m -> p t m", t=PACK))
+        nc.sync.dma_start(out=rows[0][:, FIRST_CUT:], in_=x_rows[:, 2, FIRST_CUT:])
+        pair_raw = []
+        for lo, hi in zip(PAIR_CUTS, PAIR_CUTS[1:]):
+            piece = keep.tile([P, 2, hi - lo], F32, name="pair_raw%d" % lo)
+            nc.sync.dma_start(out=piece[:], in_=x_rows[:, 0:2, lo:hi])
+            pair_raw.append((piece, lo, hi))
+        for lo, hi in zip(LAST_CUTS, LAST_CUTS[1:]):
+            nc.sync.dma_start(out=rows[1][:, lo:hi], in_=x_rows[:, 3, lo:hi])
+        w_rows = w.rearrange("(p t) m -> p t m", t=PACK)
+        w_raw = []
+        for s in range(2):
+            piece = keep.tile([P, PACK * N // 2], F32, name="w_raw%d" % s, align_bytes=64)
+            cols = slice(s * N // 2, (s + 1) * N // 2)
+            nc.sync.dma_start(out=piece[:].rearrange("p (t m) -> p t m", t=PACK), in_=w_rows[:, :, cols])
+            w_raw.append(piece)
         with nc.allow_non_contiguous_dma(reason="one bias value a partition"):
             nc.sync.dma_start(out=bias[:], in_=b.rearrange("(j p) o -> p (j o)", p=P))
 
-        singles = [keep.tile([P, T], BF16, name="single%d" % e, align_bytes=64) for e in range(2)]
-        pairs = keep.tile([P, 2 * T], BF16, name="pairs", align_bytes=64)
-        picked = keep.tile([P, D, 2, 2 * V], BF16, name="picked", align_bytes=64)
-        partial = keep.tile([P, 2, 2 * V], F32, name="partial", align_bytes=64)
-        w_bf = keep.tile([P, N * PACK], BF16, name="w_bf", align_bytes=64)
+        row_bf = [keep.tile([P, T], BF16, name="row_bf%d" % e, align_bytes=64) for e in range(2)]
+        table = keep.tile([P, 2 * T], BF16, name="table", align_bytes=64)
+        pair_picked = {
+            (d, h): keep.tile([P, 2 * HALF], BF16, name="pair_picked%d%d" % (d, h), align_bytes=64)
+            for d in range(D - 1) for h in range(2)
+        }
+        row_picked = {
+            (d, h): keep.tile([P, 2 * HALF], BF16, name="row_picked%d%d" % (d, h), align_bytes=64)
+            for d in range(D - 1) for h in range(2)
+        }
+        third = [keep.tile([P, 4 * HALF], BF16, name="third%d" % h, align_bytes=64) for h in range(2)]
+        partial0 = keep.tile([P, 4 * HALF], F32, name="partial0", align_bytes=64)
+        partial_and_w = keep.tile([P, 2 * HALF + N * PACK // 2], F32, name="partial_and_w", align_bytes=64)
+        partial = [partial0[:], partial_and_w[:, : 4 * HALF]]
+        w_bf = partial_and_w[:, 2 * HALF :].bitcast(BF16)
         x_bf0 = keep.tile([P, HALF * PACK], BF16, name="x_bf0", align_bytes=64)
-        x_bf = [x_bf0[:], w_bf[:, HALF * PACK :]]
+        x_bf = [x_bf0[:], w_raw[1][:, : HALF * PACK // 2].bitcast(BF16)]
         x_codes = keep.tile([P, V], U32, name="x_codes", align_bytes=64)
         x_scales = keep.tile([P, V], U8, name="x_scales", align_bytes=64)
         w_codes = keep.tile([P, N], U32, name="w_codes", align_bytes=64)
         w_scales = keep.tile([P, N], U8, name="w_scales", align_bytes=64)
 
-        def entries(d, v0, v1):
-            return offsets[:, (d * V + v0) // 16 : (d * V + v1) // 16]
+        def entries(d, h):
+            return offsets[:, (d * V + h * HALF) // 16 : (d * V + (h + 1) * HALF) // 16]
 
-        def gather_single(e, d, v0, v1):
-            dst = picked[:, d, 0, 2 * v0 : 2 * v1].rearrange("p (v e) -> p v e", e=2)[:, :, e]
-            nc.scalar.activation(dst, singles[e][:].indirect(entries(d, v0, v1)), COPY)
+        def row_place(e, d, h):
+            if d == D - 1:
+                return third[h][:, 2 * HALF :].rearrange("p (v e) -> p v e", e=2)[:, :, e]
+            if h == 0:
+                return row_picked[d, h][:].rearrange("p (v e) -> p v e", e=2)[:, :, e]
+            return row_picked[d, h][:, e * HALF : (e + 1) * HALF]
 
-        def gather_pair(d, v0, v1):
-            window = pairs[:].bitcast(U32).indirect(entries(d, v0, v1))
-            nc.vector.tensor_copy(out=picked[:, d, 1, 2 * v0 : 2 * v1].bitcast(U32), in_=window)
+        def gather_row(e, d, h):
+            nc.scalar.activation(row_place(e, d, h), row_bf[e][:].indirect(entries(d, h)), COPY)
 
-        def add_first(engine, u, v0, v1):
-            cols = slice(2 * v0, 2 * v1)
-            engine.tensor_tensor(partial[:, u, cols], picked[:, 0, u, cols], picked[:, 1, u, cols], ADD)
-
-        def summed(v0, v1):
-            h = v0 // HALF
-            return x_bf[h][:, PACK * (v0 - h * HALF) : PACK * (v1 - h * HALF)]
+        def gather_pair(d, h):
+            dst = third[h][:, : 2 * HALF] if d == D - 1 else pair_picked[d, h][:]
+            nc.vector.tensor_copy(out=dst.bitcast(U32), in_=table[:].bitcast(U32).indirect(entries(d, h)))
 
         def add_last(v0, v1):
-            cols = slice(2 * v0, 2 * v1)
+            h = v0 // HALF
+            ids = slice(v0 - h * HALF, v1 - h * HALF)
             nc.vector.tensor_tensor(
-                summed(v0, v1).rearrange("p (v u e) -> p v u e", u=2, e=2),
-                partial[:, :, cols].rearrange("p u (v e) -> p v u e", e=2),
-                picked[:, 2, :, cols].rearrange("p u (v e) -> p v u e", e=2),
+                x_bf[h].rearrange("p (v u e) -> p v u e", u=2, e=2)[:, ids],
+                partial[h].rearrange("p (u v e) -> p v u e", u=2, e=2)[:, ids],
+                third[h][:].rearrange("p (u v e) -> p v u e", u=2, e=2)[:, ids],
                 ADD,
             )
 
+        def cast_w(s):
+            nc.scalar.copy(
+                out=w_bf[:, s * PACK * N // 2 : (s + 1) * PACK * N // 2].rearrange("p (c i t) -> p c t i", i=4, t=PACK),
+                in_=w_raw[s][:].rearrange("p (t c i) -> p c t i", i=4, t=PACK),
+            )
+
         def quantize_x(v0, v1):
-            nc.vector.quantize_mx(out=x_codes[:, v0:v1].bitcast(FP8X4), scales=x_scales[:, v0:v1], in_=summed(v0, v1))
-
-        def cast_w(copy, s):
-            m0, m1 = s * N // 2, (s + 1) * N // 2
-            copy(
-                out=w_bf[:, PACK * m0 : PACK * m1].rearrange("p (c i t) -> p c t i", i=4, t=PACK),
-                in_=w_raw[:, :, m0:m1].rearrange("p t (c i) -> p c t i", i=4),
-            )
-
-        def quantize_w(s):
-            m0, m1 = s * N // 2, (s + 1) * N // 2
-            nc.vector.quantize_mx(
-                out=w_codes[:, m0:m1].bitcast(FP8X4), scales=w_scales[:, m0:m1], in_=w_bf[:, PACK * m0 : PACK * m1]
-            )
+            h = v0 // HALF
+            src = x_bf[h][:, PACK * (v0 - h * HALF) : PACK * (v1 - h * HALF)]
+            nc.vector.quantize_mx(out=x_codes[:, v0:v1].bitcast(FP8X4), scales=x_scales[:, v0:v1], in_=src)
 
         out_rows = out.rearrange("(j p) v -> p j v", p=P)
 
-        def multiply(acc, j, v0, v1):
-            m_cols = slice(j * P, (j + 1) * P)
-            nc.tensor.matmul_mx(
-                out=acc,
-                lhsT=w_codes[:, m_cols].bitcast(FP8X4),
-                lhsT_scale=w_scales[:, m_cols],
-                rhs=x_codes[:, v0:v1].bitcast(FP8X4),
-                rhs_scale=x_scales[:, v0:v1],
-                start=True,
-                stop=True,
-            )
+        def quantize_w(m0, m1):
+            src = w_bf[:, PACK * m0 : PACK * m1]
+            nc.vector.quantize_mx(out=w_codes[:, m0:m1].bitcast(FP8X4), scales=w_scales[:, m0:m1], in_=src)
 
-        def product(v0, v1, per_bank, on_vector, per_store):
+        def product(v0, v1, banks, on_vector, per_store):
             result = keep.tile([P, M_TILES, v1 - v0], F32, name="result%d" % v0)
-            for j0 in range(0, M_TILES, per_bank):
-                acc = psum.tile([P, per_bank, v1 - v0], F32, name="acc%d_%d" % (v0, j0))
-                for i in range(per_bank):
-                    multiply(acc[:, i, :], j0 + i, v0, v1)
-                for i in range(per_bank):
-                    j = j0 + i
-                    if j in on_vector:
-                        nc.vector.tensor_scalar(result[:, j, :], acc[:, i, :], bias[:, j : j + 1], 0.0, ADD, MAX)
-                    else:
-                        nc.scalar.activation(result[:, j, :], acc[:, i, :], RELU, bias=bias[:, j : j + 1])
-                    if (j + 1) % per_store == 0:
-                        rows = slice(j + 1 - per_store, j + 1)
-                        nc.sync.dma_start(out=out_rows[:, rows, v0:v1], in_=result[:, rows, :])
+            for j in range(M_TILES):
+                acc = psum.tile([P, v1 - v0], F32, name="acc%d_%d" % (banks, j))
+                m_cols = slice(j * P, (j + 1) * P)
+                nc.tensor.matmul_mx(
+                    out=acc[:],
+                    lhsT=w_codes[:, m_cols].bitcast(FP8X4),
+                    lhsT_scale=w_scales[:, m_cols],
+                    rhs=x_codes[:, v0:v1].bitcast(FP8X4),
+                    rhs_scale=x_scales[:, v0:v1],
+                    start=True,
+                    stop=True,
+                )
+                if j in on_vector:
+                    nc.vector.tensor_scalar(result[:, j, :], acc[:], bias[:, j : j + 1], 0.0, ADD, MAX)
+                else:
+                    nc.scalar.activation(result[:, j, :], acc[:], RELU, bias=bias[:, j : j + 1])
+                if (j + 1) % per_store == 0:
+                    tiles = slice(j + 1 - per_store, j + 1)
+                    nc.sync.dma_start(out=out_rows[:, tiles, v0:v1], in_=result[:, tiles, :])
 
-        for piece, lo, hi in early_raw:
-            nc.vector.tensor_copy(out=singles[0][:, lo:hi], in_=piece[:, 0, :])
-        for d in range(D):
-            gather_single(0, d, 0, V)
-        def cast_pair(copy, piece, lo, c0, c1):
-            copy(
-                out=pairs[:, 2 * c0 : 2 * c1].rearrange("p (c e) -> p c e", e=2),
-                in_=piece[:, :, c0 - lo : c1 - lo].rearrange("p e c -> p c e"),
-            )
-
-        for piece, lo, hi in pair_raw:
-            cast_pair(nc.vector.tensor_copy, piece, lo, lo, min(hi, T - SCALAR_SHARE))
-            if hi == T:
-                cast_pair(nc.scalar.copy, piece, lo, T - SCALAR_SHARE, T)
-        for piece, lo, hi in late_raw:
-            nc.scalar.copy(out=singles[1][:, lo:hi], in_=piece[:, 0, :])
-        for h in range(2):
-            gather_pair(0, h * HALF, (h + 1) * HALF)
-            gather_pair(1, h * HALF, (h + 1) * HALF)
-            add_first(nc.gpsimd, 1, h * HALF, (h + 1) * HALF)
-        gather_pair(2, 0, V)
+        nc.vector.tensor_copy(out=row_bf[0][:, :FIRST_CUT], in_=rows[0][:, :FIRST_CUT])
+        nc.scalar.copy(out=row_bf[0][:, FIRST_CUT:], in_=rows[0][:, FIRST_CUT:])
         for h in range(2):
             for d in range(D):
-                gather_single(1, d, h * HALF, (h + 1) * HALF)
-        add_first(nc.vector, 0, 0, HALF)
-        cast_w(nc.vector.tensor_copy, 0)
-        cast_w(nc.scalar.copy, 1)
+                gather_row(0, d, h)
+        for piece, lo, hi in pair_raw:
+            nc.vector.tensor_copy(
+                out=table[:, 2 * lo : 2 * hi].rearrange("p (c e) -> p c e", e=2),
+                in_=piece[:].rearrange("p e c -> p c e"),
+            )
+        for lo, hi in zip(LAST_CUTS, LAST_CUTS[1:]):
+            nc.scalar.copy(out=row_bf[1][:, lo:hi], in_=rows[1][:, lo:hi])
+        for h in range(2):
+            for d in range(D - 1):
+                gather_pair(d, h)
+            nc.gpsimd.tensor_tensor(partial[h][:, : 2 * HALF], pair_picked[0, h][:], pair_picked[1, h][:], ADD)
+        for h in range(2):
+            gather_pair(D - 1, h)
+        for d in range(D):
+            gather_row(1, d, 0)
+        nc.gpsimd.tensor_tensor(partial[0][:, 2 * HALF :], row_picked[0, 0][:], row_picked[1, 0][:], ADD)
+        for d in range(D - 1):
+            nc.vector.tensor_copy(out=row_place(1, d, 1), in_=rows[1][:].indirect(entries(d, 1)))
+        cast_w(0)
+        gather_row(1, D - 1, 1)
+        cast_w(1)
         add_last(0, HALF)
-        quantize_w(0)
+        quantize_w(0, N // 2)
         quantize_x(0, HALF)
-        add_first(nc.vector, 0, HALF, V)
-        quantize_w(1)
-        product(0, HALF, 2, (), 2)
+        nc.vector.tensor_tensor(
+            partial[1][:, 2 * HALF :].rearrange("p (v e) -> p v e", e=2),
+            row_picked[0, 1][:].rearrange("p (e v) -> p v e", e=2),
+            row_picked[1, 1][:].rearrange("p (e v) -> p v e", e=2),
+            ADD,
+        )
+        quantize_w(N // 2, N)
+        product(0, HALF, 0, (), 2)
         add_last(HALF, HALF + QUARTER)
         add_last(HALF + QUARTER, V)
         quantize_x(HALF, HALF + QUARTER)
         quantize_x(HALF + QUARTER, V)
-        product(HALF, HALF + QUARTER, 2, (2, 3), 4)
-        product(HALF + QUARTER, V, 1, (1, 3), 4)
+        product(HALF, HALF + QUARTER, 1, (1, 3), 2)
+        product(HALF + QUARTER, V, 0, (1, 3), 2)

@@ -21,7 +21,7 @@ PACK = 4
 HALF = V // 2
 QUARTER = V // 4
 M_TILES = N // P
-FIRST_CUT = 1536
+FIRST_CUT = 1408
 PAIR_CUTS = (0, 1152, 1728, 2048)
 LAST_CUTS = (0, 512, 1024, 1536, 2048)
 
@@ -34,21 +34,22 @@ def tile_picked_hash_lin_relu_sub_l_kernel(tc, xT, w, b, offs, out):
 
         offsets = keep.tile([P, D * V // 16], U16, name="offsets")
         bias = keep.tile([P, M_TILES], F32, name="bias")
+
+        x_rows = xT.rearrange("(p t) c -> p t c", t=PACK)
+        rows = [keep.tile([P, T], F32, name="row%d" % e) for e in range(2)]
+        nc.sync.dma_start(out=rows[0][:, : T // 2], in_=x_rows[:, 2, : T // 2])
+        nc.scalar.dma_start(out=rows[0][:, T // 2 :], in_=x_rows[:, 2, T // 2 :])
+        nc.sync.dma_start(offsets[:], offs)
+        pair_raw = []
+        for lo, hi in zip(PAIR_CUTS, PAIR_CUTS[1:]):
+            piece = keep.tile([P, 2, hi - lo], F32, name="pair_raw%d" % lo)
+            nc.scalar.dma_start(out=piece[:, 1, :], in_=x_rows[:, 1, lo:hi])
+            nc.sync.dma_start(out=piece[:, 0, :], in_=x_rows[:, 0, lo:hi])
+            pair_raw.append((piece, lo, hi))
         warm = keep.tile([P, 8], F32, name="warm")
         warm_out = keep.tile([P, 8], F32, name="warm_out")
         nc.vector.memset(warm[:], 0.0)
         nc.scalar.activation(warm_out[:], warm[:], RELU)
-
-        x_rows = xT.rearrange("(p t) c -> p t c", t=PACK)
-        rows = [keep.tile([P, T], F32, name="row%d" % e) for e in range(2)]
-        nc.sync.dma_start(out=rows[0][:, :FIRST_CUT], in_=x_rows[:, 2, :FIRST_CUT])
-        nc.sync.dma_start(offsets[:], offs)
-        nc.sync.dma_start(out=rows[0][:, FIRST_CUT:], in_=x_rows[:, 2, FIRST_CUT:])
-        pair_raw = []
-        for lo, hi in zip(PAIR_CUTS, PAIR_CUTS[1:]):
-            piece = keep.tile([P, 2, hi - lo], F32, name="pair_raw%d" % lo)
-            nc.sync.dma_start(out=piece[:], in_=x_rows[:, 0:2, lo:hi])
-            pair_raw.append((piece, lo, hi))
         for lo, hi in zip(LAST_CUTS, LAST_CUTS[1:]):
             nc.sync.dma_start(out=rows[1][:, lo:hi], in_=x_rows[:, 3, lo:hi])
         w_rows = w.rearrange("(p t) m -> p t m", t=PACK)
@@ -95,6 +96,10 @@ def tile_picked_hash_lin_relu_sub_l_kernel(tc, xT, w, b, offs, out):
 
         def gather_row(e, d, h):
             nc.scalar.activation(row_place(e, d, h), row_bf[e][:].indirect(entries(d, h)), COPY)
+
+        def gather_row_direct(e):
+            for d in range(D - 1):
+                nc.vector.tensor_copy(out=row_place(e, d, 1), in_=rows[e][:].indirect(entries(d, 1)))
 
         def gather_pair(d, h):
             dst = third[h][:, : 2 * HALF] if d == D - 1 else pair_picked[d, h][:]
@@ -151,9 +156,10 @@ def tile_picked_hash_lin_relu_sub_l_kernel(tc, xT, w, b, offs, out):
 
         nc.vector.tensor_copy(out=row_bf[0][:, :FIRST_CUT], in_=rows[0][:, :FIRST_CUT])
         nc.scalar.copy(out=row_bf[0][:, FIRST_CUT:], in_=rows[0][:, FIRST_CUT:])
-        for h in range(2):
-            for d in range(D):
-                gather_row(0, d, h)
+        for d in range(D):
+            gather_row(0, d, 0)
+        gather_row(0, D - 1, 1)
+        gather_row_direct(0)
         for piece, lo, hi in pair_raw:
             nc.vector.tensor_copy(
                 out=table[:, 2 * lo : 2 * hi].rearrange("p (c e) -> p c e", e=2),
@@ -170,8 +176,7 @@ def tile_picked_hash_lin_relu_sub_l_kernel(tc, xT, w, b, offs, out):
         for d in range(D):
             gather_row(1, d, 0)
         nc.gpsimd.tensor_tensor(partial[0][:, 2 * HALF :], row_picked[0, 0][:], row_picked[1, 0][:], ADD)
-        for d in range(D - 1):
-            nc.vector.tensor_copy(out=row_place(1, d, 1), in_=rows[1][:].indirect(entries(d, 1)))
+        gather_row_direct(1)
         cast_w(0)
         gather_row(1, D - 1, 1)
         cast_w(1)

@@ -190,10 +190,9 @@ def tile_picked_hash_lin_relu_sub_l_kernel(tc, xT, w, b, offs, out):
             ADD,
         )
         quantize_w(N // 2, N)
-        product(0, HALF, 0, (), 2)
+        product(0, HALF, 0, (), 1)
         add_last(HALF, HALF + QUARTER)
         add_last(HALF + QUARTER, V)
         quantize_x(HALF, HALF + QUARTER)
         quantize_x(HALF + QUARTER, V)
-        product(HALF, HALF + QUARTER, 1, (1, 3), 2)
-        product(HALF + QUARTER, V, 0, (1, 3), 2)
+        product(HALF, V, 1, (1, 3), 1)

@@ -46,10 +46,6 @@ def tile_picked_hash_lin_relu_sub_l_kernel(tc, xT, w, b, offs, out):
             nc.scalar.dma_start(out=piece[:, 1, :], in_=x_rows[:, 1, lo:hi])
             nc.sync.dma_start(out=piece[:, 0, :], in_=x_rows[:, 0, lo:hi])
             pair_raw.append((piece, lo, hi))
-        warm = keep.tile([P, 8], F32, name="warm")
-        warm_out = keep.tile([P, 8], F32, name="warm_out")
-        nc.vector.memset(warm[:], 0.0)
-        nc.scalar.activation(warm_out[:], warm[:], RELU)
         for lo, hi in zip(LAST_CUTS, LAST_CUTS[1:]):
             nc.sync.dma_start(out=rows[1][:, lo:hi], in_=x_rows[:, 3, lo:hi])
         w_rows = w.rearrange("(p t) m -> p t m", t=PACK)

@@ -18,11 +18,13 @@ COPY = mybir.ActivationFunctionType.Copy
 
 P = 128
 PACK = 4
+RUN = 4
 HALF = V // 2
 QUARTER = V // 4
 M_TILES = N // P
-FIRST_CUT = 1408
-PAIR_CUTS = (0, 1152, 1728, 2048)
+FIRST_CUTS = (0, 1024, 2048)
+EARLY_TILES = 2
+PAIR_PIECES = ((0, 1536, 1024), (1536, 2048, 342))
 LAST_CUTS = (0, 512, 1024, 1536, 2048)
 
 
@@ -37,15 +39,14 @@ def tile_picked_hash_lin_relu_sub_l_kernel(tc, xT, w, b, offs, out):
 
         x_rows = xT.rearrange("(p t) c -> p t c", t=PACK)
         rows = [keep.tile([P, T], F32, name="row%d" % e) for e in range(2)]
-        nc.sync.dma_start(out=rows[0][:, : T // 2], in_=x_rows[:, 2, : T // 2])
-        nc.scalar.dma_start(out=rows[0][:, T // 2 :], in_=x_rows[:, 2, T // 2 :])
+        for lo, hi in zip(FIRST_CUTS, FIRST_CUTS[1:]):
+            nc.sync.dma_start(out=rows[0][:, lo:hi], in_=x_rows[:, 2, lo:hi])
         nc.sync.dma_start(offsets[:], offs)
         pair_raw = []
-        for lo, hi in zip(PAIR_CUTS, PAIR_CUTS[1:]):
+        for lo, hi, split in PAIR_PIECES:
             piece = keep.tile([P, 2, hi - lo], F32, name="pair_raw%d" % lo)
-            nc.scalar.dma_start(out=piece[:, 1, :], in_=x_rows[:, 1, lo:hi])
-            nc.sync.dma_start(out=piece[:, 0, :], in_=x_rows[:, 0, lo:hi])
-            pair_raw.append((piece, lo, hi))
+            nc.sync.dma_start(out=piece[:], in_=x_rows[:, 0:2, lo:hi])
+            pair_raw.append(piece)
         for lo, hi in zip(LAST_CUTS, LAST_CUTS[1:]):
             nc.sync.dma_start(out=rows[1][:, lo:hi], in_=x_rows[:, 3, lo:hi])
         w_rows = w.rearrange("(p t) m -> p t m", t=PACK)
@@ -60,135 +61,140 @@ def tile_picked_hash_lin_relu_sub_l_kernel(tc, xT, w, b, offs, out):
 
         row_bf = [keep.tile([P, T], BF16, name="row_bf%d" % e, align_bytes=64) for e in range(2)]
         table = keep.tile([P, 2 * T], BF16, name="table", align_bytes=64)
+        first_picked = keep.tile([P, V], F32, name="first_picked", align_bytes=64)
         pair_picked = {
             (d, h): keep.tile([P, 2 * HALF], BF16, name="pair_picked%d%d" % (d, h), align_bytes=64)
             for d in range(D - 1) for h in range(2)
         }
-        row_picked = {
-            (d, h): keep.tile([P, 2 * HALF], BF16, name="row_picked%d%d" % (d, h), align_bytes=64)
+        last_picked = {
+            (d, h): keep.tile([P, HALF], BF16, name="last_picked%d%d" % (d, h), align_bytes=64)
             for d in range(D - 1) for h in range(2)
         }
-        third = [keep.tile([P, 4 * HALF], BF16, name="third%d" % h, align_bytes=64) for h in range(2)]
-        partial0 = keep.tile([P, 4 * HALF], F32, name="partial0", align_bytes=64)
-        partial_and_w = keep.tile([P, 2 * HALF + N * PACK // 2], F32, name="partial_and_w", align_bytes=64)
-        partial = [partial0[:], partial_and_w[:, : 4 * HALF]]
-        w_bf = partial_and_w[:, 2 * HALF :].bitcast(BF16)
-        x_bf0 = keep.tile([P, HALF * PACK], BF16, name="x_bf0", align_bytes=64)
-        x_bf = [x_bf0[:], w_raw[1][:, : HALF * PACK // 2].bitcast(BF16)]
+        third = keep.tile([P, PACK * V], BF16, name="third", align_bytes=64)
+        partial = keep.tile([P, PACK * V], F32, name="partial", align_bytes=64)
+        w_bf = [keep.tile([P, PACK * N // 2], BF16, name="w_bf%d" % s, align_bytes=64) for s in range(2)]
+        x_bf = keep.tile([P, PACK * V], BF16, name="x_bf", align_bytes=64)
         x_codes = keep.tile([P, V], U32, name="x_codes", align_bytes=64)
         x_scales = keep.tile([P, V], U8, name="x_scales", align_bytes=64)
         w_codes = keep.tile([P, N], U32, name="w_codes", align_bytes=64)
         w_scales = keep.tile([P, N], U8, name="w_scales", align_bytes=64)
 
-        def entries(d, h):
-            return offsets[:, (d * V + h * HALF) // 16 : (d * V + (h + 1) * HALF) // 16]
+        planes = partial[:].rearrange("p (t v) -> p t v", t=PACK)
+        third_runs = third[:].rearrange("p (c u i e) -> p c u i e", u=2, i=RUN, e=2)
 
-        def row_place(e, d, h):
-            if d == D - 1:
-                return third[h][:, 2 * HALF :].rearrange("p (v e) -> p v e", e=2)[:, :, e]
-            if h == 0:
-                return row_picked[d, h][:].rearrange("p (v e) -> p v e", e=2)[:, :, e]
-            return row_picked[d, h][:, e * HALF : (e + 1) * HALF]
+        def entries(d, v0, v1):
+            return offsets[:, (d * V + v0) // 16 : (d * V + v1) // 16]
 
-        def gather_row(e, d, h):
-            nc.scalar.activation(row_place(e, d, h), row_bf[e][:].indirect(entries(d, h)), COPY)
-
-        def gather_row_direct(e):
-            for d in range(D - 1):
-                nc.vector.tensor_copy(out=row_place(e, d, 1), in_=rows[e][:].indirect(entries(d, 1)))
+        def gather_third_row(e, v0, v1):
+            dst = third_runs[:, v0 // RUN : v1 // RUN, 1, :, e]
+            nc.scalar.activation(dst, row_bf[e][:].indirect(entries(D - 1, v0, v1)), COPY)
 
         def gather_pair(d, h):
-            dst = third[h][:, : 2 * HALF] if d == D - 1 else pair_picked[d, h][:]
-            nc.vector.tensor_copy(out=dst.bitcast(U32), in_=table[:].bitcast(U32).indirect(entries(d, h)))
+            src = table[:].bitcast(U32).indirect(entries(d, h * HALF, (h + 1) * HALF))
+            nc.vector.tensor_copy(out=pair_picked[d, h][:].bitcast(U32), in_=src)
 
         def add_last(v0, v1):
-            h = v0 // HALF
-            ids = slice(v0 - h * HALF, v1 - h * HALF)
+            blocks = slice(v0 // RUN, v1 // RUN)
             nc.vector.tensor_tensor(
-                x_bf[h].rearrange("p (v u e) -> p v u e", u=2, e=2)[:, ids],
-                partial[h].rearrange("p (u v e) -> p v u e", u=2, e=2)[:, ids],
-                third[h][:].rearrange("p (u v e) -> p v u e", u=2, e=2)[:, ids],
+                x_bf[:].rearrange("p (c i u e) -> p c u e i", i=RUN, u=2, e=2)[:, blocks],
+                partial[:].rearrange("p (u e c i) -> p c u e i", u=2, e=2, i=RUN)[:, blocks],
+                third[:].rearrange("p (c u i e) -> p c u e i", u=2, i=RUN, e=2)[:, blocks],
                 ADD,
             )
 
         def cast_w(s):
             nc.scalar.copy(
-                out=w_bf[:, s * PACK * N // 2 : (s + 1) * PACK * N // 2].rearrange("p (c i t) -> p c t i", i=4, t=PACK),
+                out=w_bf[s][:].rearrange("p (c i t) -> p c t i", i=4, t=PACK),
                 in_=w_raw[s][:].rearrange("p (t c i) -> p c t i", i=4, t=PACK),
             )
 
+        def quantize_w(s):
+            cols = slice(s * N // 2, (s + 1) * N // 2)
+            nc.vector.quantize_mx(out=w_codes[:, cols].bitcast(FP8X4), scales=w_scales[:, cols], in_=w_bf[s][:])
+
         def quantize_x(v0, v1):
-            h = v0 // HALF
-            src = x_bf[h][:, PACK * (v0 - h * HALF) : PACK * (v1 - h * HALF)]
+            src = x_bf[:, PACK * v0 : PACK * v1]
             nc.vector.quantize_mx(out=x_codes[:, v0:v1].bitcast(FP8X4), scales=x_scales[:, v0:v1], in_=src)
 
         out_rows = out.rearrange("(j p) v -> p j v", p=P)
 
-        def quantize_w(m0, m1):
-            src = w_bf[:, PACK * m0 : PACK * m1]
-            nc.vector.quantize_mx(out=w_codes[:, m0:m1].bitcast(FP8X4), scales=w_scales[:, m0:m1], in_=src)
+        banks = [psum.tile([P, HALF], F32, name="bank%d" % n) for n in range(2 * M_TILES)]
 
-        def product(v0, v1, banks, on_vector, per_store):
-            result = keep.tile([P, M_TILES, v1 - v0], F32, name="result%d" % v0)
-            for j in range(M_TILES):
-                acc = psum.tile([P, v1 - v0], F32, name="acc%d_%d" % (banks, j))
-                m_cols = slice(j * P, (j + 1) * P)
-                nc.tensor.matmul_mx(
-                    out=acc[:],
-                    lhsT=w_codes[:, m_cols].bitcast(FP8X4),
-                    lhsT_scale=w_scales[:, m_cols],
-                    rhs=x_codes[:, v0:v1].bitcast(FP8X4),
-                    rhs_scale=x_scales[:, v0:v1],
-                    start=True,
-                    stop=True,
-                )
-                if j in on_vector:
-                    nc.vector.tensor_scalar(result[:, j, :], acc[:], bias[:, j : j + 1], 0.0, ADD, MAX)
-                else:
-                    nc.scalar.activation(result[:, j, :], acc[:], RELU, bias=bias[:, j : j + 1])
-                if (j + 1) % per_store == 0:
-                    tiles = slice(j + 1 - per_store, j + 1)
-                    nc.sync.dma_start(out=out_rows[:, tiles, v0:v1], in_=result[:, tiles, :])
-
-        nc.vector.tensor_copy(out=row_bf[0][:, :FIRST_CUT], in_=rows[0][:, :FIRST_CUT])
-        nc.scalar.copy(out=row_bf[0][:, FIRST_CUT:], in_=rows[0][:, FIRST_CUT:])
-        for d in range(D):
-            gather_row(0, d, 0)
-        gather_row(0, D - 1, 1)
-        gather_row_direct(0)
-        for piece, lo, hi in pair_raw:
-            nc.vector.tensor_copy(
-                out=table[:, 2 * lo : 2 * hi].rearrange("p (c e) -> p c e", e=2),
-                in_=piece[:].rearrange("p e c -> p c e"),
+        def multiply(acc, j, v0, v1):
+            m_cols = slice(j * P, (j + 1) * P)
+            nc.tensor.matmul_mx(
+                out=acc,
+                lhsT=w_codes[:, m_cols].bitcast(FP8X4),
+                lhsT_scale=w_scales[:, m_cols],
+                rhs=x_codes[:, v0:v1].bitcast(FP8X4),
+                rhs_scale=x_scales[:, v0:v1],
+                start=True,
+                stop=True,
             )
+
+        def finish(acc, j, v0, v1, on_vector):
+            result = keep.tile([P, v1 - v0], F32, name="result%d_%d" % (v0, j))
+            if on_vector:
+                nc.vector.tensor_scalar(result[:], acc, bias[:, j : j + 1], 0.0, ADD, MAX)
+            else:
+                nc.scalar.activation(result[:], acc, RELU, bias=bias[:, j : j + 1])
+            nc.sync.dma_start(out=out_rows[:, j, v0:v1], in_=result[:])
+
+        for lo, hi in zip(FIRST_CUTS, FIRST_CUTS[1:]):
+            nc.scalar.copy(out=row_bf[0][:, lo:hi], in_=rows[0][:, lo:hi])
+        nc.vector.tensor_copy(out=first_picked[:], in_=rows[0][:].indirect(entries(0, 0, V)))
+        nc.vector.tensor_tensor(planes[:, 2, :], rows[0][:].indirect(entries(1, 0, V)), first_picked[:], ADD)
+        gather_third_row(0, 0, V)
+        for piece, (lo, hi, split) in zip(pair_raw, PAIR_PIECES):
+            words = table[:, 2 * lo : 2 * hi].rearrange("p (c e) -> p c e", e=2)
+            src = piece[:].rearrange("p e c -> p c e")
+            nc.vector.tensor_copy(out=words[:, :split], in_=src[:, :split])
+            nc.scalar.copy(out=words[:, split:], in_=src[:, split:])
         for lo, hi in zip(LAST_CUTS, LAST_CUTS[1:]):
             nc.scalar.copy(out=row_bf[1][:, lo:hi], in_=rows[1][:, lo:hi])
         for h in range(2):
             for d in range(D - 1):
                 gather_pair(d, h)
-            nc.gpsimd.tensor_tensor(partial[h][:, : 2 * HALF], pair_picked[0, h][:], pair_picked[1, h][:], ADD)
-        for h in range(2):
-            gather_pair(D - 1, h)
-        for d in range(D):
-            gather_row(1, d, 0)
-        nc.gpsimd.tensor_tensor(partial[0][:, 2 * HALF :], row_picked[0, 0][:], row_picked[1, 0][:], ADD)
-        gather_row_direct(1)
-        cast_w(0)
-        gather_row(1, D - 1, 1)
-        cast_w(1)
-        add_last(0, HALF)
-        quantize_w(0, N // 2)
-        quantize_x(0, HALF)
-        nc.vector.tensor_tensor(
-            partial[1][:, 2 * HALF :].rearrange("p (v e) -> p v e", e=2),
-            row_picked[0, 1][:].rearrange("p (e v) -> p v e", e=2),
-            row_picked[1, 1][:].rearrange("p (e v) -> p v e", e=2),
-            ADD,
+            nc.gpsimd.tensor_tensor(
+                planes[:, 0:2, h * HALF : (h + 1) * HALF],
+                pair_picked[0, h][:].rearrange("p (v e) -> p e v", e=2),
+                pair_picked[1, h][:].rearrange("p (v e) -> p e v", e=2),
+                ADD,
+            )
+        nc.vector.tensor_copy(
+            out=third[:].bitcast(U32).rearrange("p (c u i) -> p c u i", u=2, i=RUN)[:, :, 0, :],
+            in_=table[:].bitcast(U32).indirect(entries(D - 1, 0, V)),
         )
-        quantize_w(N // 2, N)
-        product(0, HALF, 0, (), 1)
-        add_last(HALF, HALF + QUARTER)
-        add_last(HALF + QUARTER, V)
-        quantize_x(HALF, HALF + QUARTER)
-        quantize_x(HALF + QUARTER, V)
-        product(HALF, V, 1, (1, 3), 1)
+        for d in range(D - 1):
+            nc.scalar.activation(last_picked[d, 0][:], row_bf[1][:].indirect(entries(d, 0, HALF)), COPY)
+        gather_third_row(1, 0, HALF)
+        nc.gpsimd.tensor_tensor(planes[:, 3, :HALF], last_picked[0, 0][:], last_picked[1, 0][:], ADD)
+        for d in range(D - 1):
+            nc.vector.tensor_copy(out=last_picked[d, 1][:], in_=rows[1][:].indirect(entries(d, HALF, V)))
+        cast_w(0)
+        cast_w(1)
+        gather_third_row(1, HALF, V)
+        add_last(0, HALF)
+        quantize_w(0)
+        quantize_x(0, HALF)
+        nc.vector.tensor_tensor(planes[:, 3, HALF:], last_picked[0, 1][:], last_picked[1, 1][:], ADD)
+        quantize_w(1)
+        for j in range(M_TILES):
+            multiply(banks[j][:], j, 0, HALF)
+            finish(banks[j][:], j, 0, HALF, False)
+        last = HALF + QUARTER
+        add_last(HALF, last)
+        add_last(last, V)
+        quantize_x(HALF, last)
+        quantize_x(last, V)
+        for j in range(M_TILES):
+            multiply(banks[M_TILES + j][:, :QUARTER], j, HALF, last)
+            if j < EARLY_TILES:
+                finish(banks[M_TILES + j][:, :QUARTER], j, HALF, last, False)
+        for j in range(M_TILES):
+            if j < EARLY_TILES:
+                multiply(banks[j][:, :QUARTER], j, last, V)
+                finish(banks[j][:, :QUARTER], j, last, V, j % 2 == 0)
+            else:
+                multiply(banks[M_TILES + j][:, QUARTER:], j, last, V)
+                finish(banks[M_TILES + j][:], j, HALF, V, j % 2 == 0)

@@ -71,15 +71,17 @@ def tile_picked_hash_lin_relu_sub_l_kernel(tc, xT, w, b, offs, out):
             for d in range(D - 1) for h in range(2)
         }
         third = keep.tile([P, PACK * V], BF16, name="third", align_bytes=64)
-        partial = keep.tile([P, PACK * V], F32, name="partial", align_bytes=64)
-        w_bf = [keep.tile([P, PACK * N // 2], BF16, name="w_bf%d" % s, align_bytes=64) for s in range(2)]
+        partial_and_w = keep.tile([P, PACK * V + HALF], F32, name="partial_and_w", align_bytes=64)
+        partial = partial_and_w[:, : PACK * V]
+        w_bf1 = keep.tile([P, PACK * N // 2], BF16, name="w_bf1", align_bytes=64)
+        w_bf = [partial_and_w[:, PACK * V - HALF :].bitcast(BF16), w_bf1[:]]
         x_bf = keep.tile([P, PACK * V], BF16, name="x_bf", align_bytes=64)
         x_codes = keep.tile([P, V], U32, name="x_codes", align_bytes=64)
         x_scales = keep.tile([P, V], U8, name="x_scales", align_bytes=64)
         w_codes = keep.tile([P, N], U32, name="w_codes", align_bytes=64)
         w_scales = keep.tile([P, N], U8, name="w_scales", align_bytes=64)
 
-        planes = partial[:].rearrange("p (t v) -> p t v", t=PACK)
+        planes = partial.rearrange("p (t v) -> p t v", t=PACK)
         third_runs = third[:].rearrange("p (c u i e) -> p c u i e", u=2, i=RUN, e=2)
 
         def entries(d, v0, v1):
@@ -97,20 +99,20 @@ def tile_picked_hash_lin_relu_sub_l_kernel(tc, xT, w, b, offs, out):
             blocks = slice(v0 // RUN, v1 // RUN)
             nc.vector.tensor_tensor(
                 x_bf[:].rearrange("p (c i u e) -> p c u e i", i=RUN, u=2, e=2)[:, blocks],
-                partial[:].rearrange("p (u e c i) -> p c u e i", u=2, e=2, i=RUN)[:, blocks],
+                partial.rearrange("p (u e c i) -> p c u e i", u=2, e=2, i=RUN)[:, blocks],
                 third[:].rearrange("p (c u i e) -> p c u e i", u=2, i=RUN, e=2)[:, blocks],
                 ADD,
             )
 
         def cast_w(s):
             nc.scalar.copy(
-                out=w_bf[s][:].rearrange("p (c i t) -> p c t i", i=4, t=PACK),
+                out=w_bf[s].rearrange("p (c i t) -> p c t i", i=4, t=PACK),
                 in_=w_raw[s][:].rearrange("p (t c i) -> p c t i", i=4, t=PACK),
             )
 
         def quantize_w(s):
             cols = slice(s * N // 2, (s + 1) * N // 2)
-            nc.vector.quantize_mx(out=w_codes[:, cols].bitcast(FP8X4), scales=w_scales[:, cols], in_=w_bf[s][:])
+            nc.vector.quantize_mx(out=w_codes[:, cols].bitcast(FP8X4), scales=w_scales[:, cols], in_=w_bf[s])
 
         def quantize_x(v0, v1):
             src = x_bf[:, PACK * v0 : PACK * v1]

@@ -22,10 +22,7 @@ RUN = 4
 HALF = V // 2
 QUARTER = V // 4
 M_TILES = N // P
-FIRST_CUTS = (0, 1024, 2048)
 EARLY_TILES = 2
-PAIR_PIECES = ((0, 1536, 1024), (1536, 2048, 342))
-LAST_CUTS = (0, 512, 1024, 1536, 2048)
 
 
 def tile_picked_hash_lin_relu_sub_l_kernel(tc, xT, w, b, offs, out):
@@ -38,17 +35,11 @@ def tile_picked_hash_lin_relu_sub_l_kernel(tc, xT, w, b, offs, out):
         bias = keep.tile([P, M_TILES], F32, name="bias")
 
         x_rows = xT.rearrange("(p t) c -> p t c", t=PACK)
-        rows = [keep.tile([P, T], F32, name="row%d" % e) for e in range(2)]
-        for lo, hi in zip(FIRST_CUTS, FIRST_CUTS[1:]):
-            nc.sync.dma_start(out=rows[0][:, lo:hi], in_=x_rows[:, 2, lo:hi])
+        rows = [keep.tile([P, T], F32, name="row%d" % t) for t in range(PACK)]
+        nc.sync.dma_start(out=rows[0][:], in_=x_rows[:, 0, :])
         nc.sync.dma_start(offsets[:], offs)
-        pair_raw = []
-        for lo, hi, split in PAIR_PIECES:
-            piece = keep.tile([P, 2, hi - lo], F32, name="pair_raw%d" % lo)
-            nc.sync.dma_start(out=piece[:], in_=x_rows[:, 0:2, lo:hi])
-            pair_raw.append(piece)
-        for lo, hi in zip(LAST_CUTS, LAST_CUTS[1:]):
-            nc.sync.dma_start(out=rows[1][:, lo:hi], in_=x_rows[:, 3, lo:hi])
+        for t in range(1, PACK):
+            nc.sync.dma_start(out=rows[t][:], in_=x_rows[:, t, :])
         w_rows = w.rearrange("(p t) m -> p t m", t=PACK)
         w_raw = []
         for s in range(2):
@@ -59,67 +50,46 @@ def tile_picked_hash_lin_relu_sub_l_kernel(tc, xT, w, b, offs, out):
         with nc.allow_non_contiguous_dma(reason="one bias value a partition"):
             nc.sync.dma_start(out=bias[:], in_=b.rearrange("(j p) o -> p (j o)", p=P))
 
-        row_bf = [keep.tile([P, T], BF16, name="row_bf%d" % e, align_bytes=64) for e in range(2)]
-        table = keep.tile([P, 2 * T], BF16, name="table", align_bytes=64)
-        first_picked = keep.tile([P, V], F32, name="first_picked", align_bytes=64)
-        pair_picked = {
-            (d, h): keep.tile([P, 2 * HALF], BF16, name="pair_picked%d%d" % (d, h), align_bytes=64)
-            for d in range(D - 1) for h in range(2)
-        }
-        last_picked = {
-            (d, h): keep.tile([P, HALF], BF16, name="last_picked%d%d" % (d, h), align_bytes=64)
-            for d in range(D - 1) for h in range(2)
-        }
-        third = keep.tile([P, PACK * V], BF16, name="third", align_bytes=64)
-        partial_and_w = keep.tile([P, PACK * V + HALF], F32, name="partial_and_w", align_bytes=64)
-        partial = partial_and_w[:, : PACK * V]
-        w_bf1 = keep.tile([P, PACK * N // 2], BF16, name="w_bf1", align_bytes=64)
-        w_bf = [partial_and_w[:, PACK * V - HALF :].bitcast(BF16), w_bf1[:]]
+        first = keep.tile([P, PACK * V], F32, name="first", align_bytes=64)
+        partial = keep.tile([P, PACK * V], F32, name="partial", align_bytes=64)
+        third = keep.tile([P, PACK * V], F32, name="third", align_bytes=64)
+        w_bf = [keep.tile([P, PACK * N // 2], BF16, name="w_bf%d" % s, align_bytes=64) for s in range(2)]
         x_bf = keep.tile([P, PACK * V], BF16, name="x_bf", align_bytes=64)
         x_codes = keep.tile([P, V], U32, name="x_codes", align_bytes=64)
         x_scales = keep.tile([P, V], U8, name="x_scales", align_bytes=64)
         w_codes = keep.tile([P, N], U32, name="w_codes", align_bytes=64)
         w_scales = keep.tile([P, N], U8, name="w_scales", align_bytes=64)
 
-        planes = partial.rearrange("p (t v) -> p t v", t=PACK)
-        third_runs = third[:].rearrange("p (c u i e) -> p c u i e", u=2, i=RUN, e=2)
+        def picked(t, d, v0, v1):
+            return rows[t][:].indirect(offsets[:, (d * V + v0) // 16 : (d * V + v1) // 16])
 
-        def entries(d, v0, v1):
-            return offsets[:, (d * V + v0) // 16 : (d * V + v1) // 16]
-
-        def gather_third_row(e, v0, v1):
-            dst = third_runs[:, v0 // RUN : v1 // RUN, 1, :, e]
-            nc.scalar.activation(dst, row_bf[e][:].indirect(entries(D - 1, v0, v1)), COPY)
-
-        def gather_pair(d, h):
-            src = table[:].bitcast(U32).indirect(entries(d, h * HALF, (h + 1) * HALF))
-            nc.vector.tensor_copy(out=pair_picked[d, h][:].bitcast(U32), in_=src)
+        def plane(tile, t, v0, v1):
+            return tile[:, t * V + v0 : t * V + v1]
 
         def add_last(v0, v1):
             blocks = slice(v0 // RUN, v1 // RUN)
             nc.vector.tensor_tensor(
-                x_bf[:].rearrange("p (c i u e) -> p c u e i", i=RUN, u=2, e=2)[:, blocks],
-                partial.rearrange("p (u e c i) -> p c u e i", u=2, e=2, i=RUN)[:, blocks],
-                third[:].rearrange("p (c u i e) -> p c u e i", u=2, i=RUN, e=2)[:, blocks],
+                x_bf[:].rearrange("p (c i t) -> p c t i", i=RUN, t=PACK)[:, blocks],
+                partial[:].rearrange("p (t c i) -> p c t i", t=PACK, i=RUN)[:, blocks],
+                third[:].rearrange("p (t c i) -> p c t i", t=PACK, i=RUN)[:, blocks],
                 ADD,
             )
 
         def cast_w(s):
             nc.scalar.copy(
-                out=w_bf[s].rearrange("p (c i t) -> p c t i", i=4, t=PACK),
-                in_=w_raw[s][:].rearrange("p (t c i) -> p c t i", i=4, t=PACK),
+                out=w_bf[s][:].rearrange("p (c i t) -> p c t i", i=RUN, t=PACK),
+                in_=w_raw[s][:].rearrange("p (t c i) -> p c t i", i=RUN, t=PACK),
             )
 
         def quantize_w(s):
             cols = slice(s * N // 2, (s + 1) * N // 2)
-            nc.vector.quantize_mx(out=w_codes[:, cols].bitcast(FP8X4), scales=w_scales[:, cols], in_=w_bf[s])
+            nc.vector.quantize_mx(out=w_codes[:, cols].bitcast(FP8X4), scales=w_scales[:, cols], in_=w_bf[s][:])
 
         def quantize_x(v0, v1):
             src = x_bf[:, PACK * v0 : PACK * v1]
             nc.vector.quantize_mx(out=x_codes[:, v0:v1].bitcast(FP8X4), scales=x_scales[:, v0:v1], in_=src)
 
         out_rows = out.rearrange("(j p) v -> p j v", p=P)
-
         banks = [psum.tile([P, HALF], F32, name="bank%d" % n) for n in range(2 * M_TILES)]
 
         def multiply(acc, j, v0, v1):
@@ -142,51 +112,31 @@ def tile_picked_hash_lin_relu_sub_l_kernel(tc, xT, w, b, offs, out):
                 nc.scalar.activation(result[:], acc, RELU, bias=bias[:, j : j + 1])
             nc.sync.dma_start(out=out_rows[:, j, v0:v1], in_=result[:])
 
-        for lo, hi in zip(FIRST_CUTS, FIRST_CUTS[1:]):
-            nc.scalar.copy(out=row_bf[0][:, lo:hi], in_=rows[0][:, lo:hi])
-        nc.vector.tensor_copy(out=first_picked[:], in_=rows[0][:].indirect(entries(0, 0, V)))
-        nc.vector.tensor_tensor(planes[:, 2, :], rows[0][:].indirect(entries(1, 0, V)), first_picked[:], ADD)
-        gather_third_row(0, 0, V)
-        for piece, (lo, hi, split) in zip(pair_raw, PAIR_PIECES):
-            words = table[:, 2 * lo : 2 * hi].rearrange("p (c e) -> p c e", e=2)
-            src = piece[:].rearrange("p e c -> p c e")
-            nc.vector.tensor_copy(out=words[:, :split], in_=src[:, :split])
-            nc.scalar.copy(out=words[:, split:], in_=src[:, split:])
-        for lo, hi in zip(LAST_CUTS, LAST_CUTS[1:]):
-            nc.scalar.copy(out=row_bf[1][:, lo:hi], in_=rows[1][:, lo:hi])
-        for h in range(2):
-            for d in range(D - 1):
-                gather_pair(d, h)
-            nc.gpsimd.tensor_tensor(
-                planes[:, 0:2, h * HALF : (h + 1) * HALF],
-                pair_picked[0, h][:].rearrange("p (v e) -> p e v", e=2),
-                pair_picked[1, h][:].rearrange("p (v e) -> p e v", e=2),
-                ADD,
-            )
-        nc.vector.tensor_copy(
-            out=third[:].bitcast(U32).rearrange("p (c u i) -> p c u i", u=2, i=RUN)[:, :, 0, :],
-            in_=table[:].bitcast(U32).indirect(entries(D - 1, 0, V)),
-        )
-        for d in range(D - 1):
-            nc.scalar.activation(last_picked[d, 0][:], row_bf[1][:].indirect(entries(d, 0, HALF)), COPY)
-        gather_third_row(1, 0, HALF)
-        nc.gpsimd.tensor_tensor(planes[:, 3, :HALF], last_picked[0, 0][:], last_picked[1, 0][:], ADD)
-        for d in range(D - 1):
-            nc.vector.tensor_copy(out=last_picked[d, 1][:], in_=rows[1][:].indirect(entries(d, HALF, V)))
+        warm_in = keep.tile([P, 1], F32, name="warm_in")
+        warm_out = keep.tile([P, 1], F32, name="warm_out")
+        nc.vector.memset(warm_in[:], 0.0)
+        nc.scalar.activation(warm_out[:], warm_in[:], COPY)
+
+        for t in range(PACK):
+            spans = [(0, V)] if t < PACK - 2 else [(0, HALF), (HALF, V)]
+            for v0, v1 in spans:
+                nc.scalar.activation(plane(first, t, v0, v1), picked(t, 0, v0, v1), COPY)
+            nc.scalar.activation(plane(third, t, HALF, V), picked(t, 2, HALF, V), COPY)
+            nc.vector.tensor_copy(out=plane(third, t, 0, HALF), in_=picked(t, 2, 0, HALF))
+            for v0, v1 in spans:
+                nc.vector.tensor_tensor(plane(partial, t, v0, v1), picked(t, 1, v0, v1), plane(first, t, v0, v1), ADD)
         cast_w(0)
         cast_w(1)
-        gather_third_row(1, HALF, V)
+        last = HALF + QUARTER
         add_last(0, HALF)
         quantize_w(0)
         quantize_x(0, HALF)
-        nc.vector.tensor_tensor(planes[:, 3, HALF:], last_picked[0, 1][:], last_picked[1, 1][:], ADD)
+        add_last(HALF, last)
         quantize_w(1)
+        add_last(last, V)
         for j in range(M_TILES):
             multiply(banks[j][:], j, 0, HALF)
             finish(banks[j][:], j, 0, HALF, False)
-        last = HALF + QUARTER
-        add_last(HALF, last)
-        add_last(last, V)
         quantize_x(HALF, last)
         quantize_x(last, V)
         for j in range(M_TILES):

@@ -22,7 +22,6 @@ RUN = 4
 HALF = V // 2
 QUARTER = V // 4
 M_TILES = N // P
-EARLY_TILES = 2
 
 
 def tile_picked_hash_lin_relu_sub_l_kernel(tc, xT, w, b, offs, out):
@@ -41,19 +40,19 @@ def tile_picked_hash_lin_relu_sub_l_kernel(tc, xT, w, b, offs, out):
         for t in range(1, PACK):
             nc.sync.dma_start(out=rows[t][:], in_=x_rows[:, t, :])
         w_rows = w.rearrange("(p t) m -> p t m", t=PACK)
-        w_raw = []
+        w_raw0 = keep.tile([P, PACK * N // 2], F32, name="w_raw0", align_bytes=64)
+        third_and_w = keep.tile([P, PACK * V - QUARTER + PACK * N // 2], F32, name="third_and_w", align_bytes=64)
+        third = third_and_w[:, : PACK * V]
+        w_raw = [w_raw0[:], third_and_w[:, PACK * V - QUARTER :]]
         for s in range(2):
-            piece = keep.tile([P, PACK * N // 2], F32, name="w_raw%d" % s, align_bytes=64)
             cols = slice(s * N // 2, (s + 1) * N // 2)
-            nc.sync.dma_start(out=piece[:].rearrange("p (t m) -> p t m", t=PACK), in_=w_rows[:, :, cols])
-            w_raw.append(piece)
+            nc.sync.dma_start(out=w_raw[s].rearrange("p (t m) -> p t m", t=PACK), in_=w_rows[:, :, cols])
         with nc.allow_non_contiguous_dma(reason="one bias value a partition"):
             nc.sync.dma_start(out=bias[:], in_=b.rearrange("(j p) o -> p (j o)", p=P))
 
         first = keep.tile([P, PACK * V], F32, name="first", align_bytes=64)
         partial = keep.tile([P, PACK * V], F32, name="partial", align_bytes=64)
-        third = keep.tile([P, PACK * V], F32, name="third", align_bytes=64)
-        w_bf = [keep.tile([P, PACK * N // 2], BF16, name="w_bf%d" % s, align_bytes=64) for s in range(2)]
+        w_bf = keep.tile([P, PACK * N], BF16, name="w_bf", align_bytes=64)
         x_bf = keep.tile([P, PACK * V], BF16, name="x_bf", align_bytes=64)
         x_codes = keep.tile([P, V], U32, name="x_codes", align_bytes=64)
         x_scales = keep.tile([P, V], U8, name="x_scales", align_bytes=64)
@@ -71,19 +70,21 @@ def tile_picked_hash_lin_relu_sub_l_kernel(tc, xT, w, b, offs, out):
             nc.vector.tensor_tensor(
                 x_bf[:].rearrange("p (c i t) -> p c t i", i=RUN, t=PACK)[:, blocks],
                 partial[:].rearrange("p (t c i) -> p c t i", t=PACK, i=RUN)[:, blocks],
-                third[:].rearrange("p (t c i) -> p c t i", t=PACK, i=RUN)[:, blocks],
+                third.rearrange("p (t c i) -> p c t i", t=PACK, i=RUN)[:, blocks],
                 ADD,
             )
 
-        def cast_w(s):
+        def cast_w(m0, m1):
+            raw = w_raw[2 * m0 // N].rearrange("p (t c i) -> p c t i", i=RUN, t=PACK)
+            start = m0 % (N // 2)
             nc.scalar.copy(
-                out=w_bf[s][:].rearrange("p (c i t) -> p c t i", i=RUN, t=PACK),
-                in_=w_raw[s][:].rearrange("p (t c i) -> p c t i", i=RUN, t=PACK),
+                out=w_bf[:, PACK * m0 : PACK * m1].rearrange("p (c i t) -> p c t i", i=RUN, t=PACK),
+                in_=raw[:, start // RUN : (start + m1 - m0) // RUN],
             )
 
-        def quantize_w(s):
-            cols = slice(s * N // 2, (s + 1) * N // 2)
-            nc.vector.quantize_mx(out=w_codes[:, cols].bitcast(FP8X4), scales=w_scales[:, cols], in_=w_bf[s][:])
+        def quantize_w(m0, m1):
+            src = w_bf[:, PACK * m0 : PACK * m1]
+            nc.vector.quantize_mx(out=w_codes[:, m0:m1].bitcast(FP8X4), scales=w_scales[:, m0:m1], in_=src)
 
         def quantize_x(v0, v1):
             src = x_bf[:, PACK * v0 : PACK * v1]
@@ -117,36 +118,35 @@ def tile_picked_hash_lin_relu_sub_l_kernel(tc, xT, w, b, offs, out):
         nc.vector.memset(warm_in[:], 0.0)
         nc.scalar.activation(warm_out[:], warm_in[:], COPY)
 
+        last = HALF + QUARTER
         for t in range(PACK):
             spans = [(0, V)] if t < PACK - 2 else [(0, HALF), (HALF, V)]
             for v0, v1 in spans:
                 nc.scalar.activation(plane(first, t, v0, v1), picked(t, 0, v0, v1), COPY)
-            nc.scalar.activation(plane(third, t, HALF, V), picked(t, 2, HALF, V), COPY)
+            end = V if t < PACK - 1 else last
+            nc.scalar.activation(plane(third, t, HALF, end), picked(t, 2, HALF, end), COPY)
             nc.vector.tensor_copy(out=plane(third, t, 0, HALF), in_=picked(t, 2, 0, HALF))
             for v0, v1 in spans:
                 nc.vector.tensor_tensor(plane(partial, t, v0, v1), picked(t, 1, v0, v1), plane(first, t, v0, v1), ADD)
-        cast_w(0)
-        cast_w(1)
-        last = HALF + QUARTER
+        for j in range(3):
+            cast_w(j * P, (j + 1) * P)
+        nc.scalar.activation(plane(third, PACK - 1, last, V), picked(PACK - 1, 2, last, V), COPY)
+        cast_w(3 * P, N)
         add_last(0, HALF)
-        quantize_w(0)
+        quantize_w(0, P)
         quantize_x(0, HALF)
+        quantize_w(P, 2 * P)
         add_last(HALF, last)
-        quantize_w(1)
+        quantize_w(2 * P, 3 * P)
+        quantize_x(HALF, last)
         add_last(last, V)
+        quantize_w(3 * P, N)
+        quantize_x(last, V)
         for j in range(M_TILES):
             multiply(banks[j][:], j, 0, HALF)
             finish(banks[j][:], j, 0, HALF, False)
-        quantize_x(HALF, last)
-        quantize_x(last, V)
         for j in range(M_TILES):
             multiply(banks[M_TILES + j][:, :QUARTER], j, HALF, last)
-            if j < EARLY_TILES:
-                finish(banks[M_TILES + j][:, :QUARTER], j, HALF, last, False)
         for j in range(M_TILES):
-            if j < EARLY_TILES:
-                multiply(banks[j][:, :QUARTER], j, last, V)
-                finish(banks[j][:, :QUARTER], j, last, V, j % 2 == 0)
-            else:
-                multiply(banks[M_TILES + j][:, QUARTER:], j, last, V)
-                finish(banks[M_TILES + j][:], j, HALF, V, j % 2 == 0)
+            multiply(banks[M_TILES + j][:, QUARTER:], j, last, V)
+            finish(banks[M_TILES + j][:], j, HALF, V, j % 2 == 0)

@@ -50,10 +50,13 @@ def tile_picked_hash_lin_relu_sub_l_kernel(tc, xT, w, b, offs, out):
         with nc.allow_non_contiguous_dma(reason="one bias value a partition"):
             nc.sync.dma_start(out=bias[:], in_=b.rearrange("(j p) o -> p (j o)", p=P))
 
-        first = keep.tile([P, PACK * V], F32, name="first", align_bytes=64)
+        early_low = keep.tile([P, 2, HALF], F32, name="early_low", align_bytes=64)
+        early_high = keep.tile([P, 2 * HALF], F32, name="early_high", align_bytes=64)
+        late_first = [keep.tile([P, V], F32, name="late_first%d" % t, align_bytes=64) for t in range(2)]
         partial = keep.tile([P, PACK * V], F32, name="partial", align_bytes=64)
         w_bf = keep.tile([P, PACK * N], BF16, name="w_bf", align_bytes=64)
-        x_bf = keep.tile([P, PACK * V], BF16, name="x_bf", align_bytes=64)
+        x_bf1 = keep.tile([P, PACK * HALF], BF16, name="x_bf1", align_bytes=64)
+        x_bf = [early_high[:].bitcast(BF16), x_bf1[:]]
         x_codes = keep.tile([P, V], U32, name="x_codes", align_bytes=64)
         x_scales = keep.tile([P, V], U8, name="x_scales", align_bytes=64)
         w_codes = keep.tile([P, N], U32, name="w_codes", align_bytes=64)
@@ -65,12 +68,21 @@ def tile_picked_hash_lin_relu_sub_l_kernel(tc, xT, w, b, offs, out):
         def plane(tile, t, v0, v1):
             return tile[:, t * V + v0 : t * V + v1]
 
-        def add_last(v0, v1):
+        def first_half(t, v0):
+            if t >= 2:
+                return late_first[t - 2][:, v0 : v0 + HALF]
+            return early_high[:, t * HALF : (t + 1) * HALF] if v0 else early_low[:, t, :]
+
+        def rounded(v0, v1):
+            h = v0 // HALF
+            return x_bf[h][:, PACK * (v0 - h * HALF) : PACK * (v1 - h * HALF)]
+
+        def add_last(engine, t0, t1, v0, v1):
             blocks = slice(v0 // RUN, v1 // RUN)
-            nc.vector.tensor_tensor(
-                x_bf[:].rearrange("p (c i t) -> p c t i", i=RUN, t=PACK)[:, blocks],
-                partial[:].rearrange("p (t c i) -> p c t i", t=PACK, i=RUN)[:, blocks],
-                third.rearrange("p (t c i) -> p c t i", t=PACK, i=RUN)[:, blocks],
+            engine.tensor_tensor(
+                rounded(v0, v1).rearrange("p (c i t) -> p c t i", i=RUN, t=PACK)[:, :, t0:t1],
+                partial[:].rearrange("p (t c i) -> p c t i", t=PACK, i=RUN)[:, blocks, t0:t1],
+                third.rearrange("p (t c i) -> p c t i", t=PACK, i=RUN)[:, blocks, t0:t1],
                 ADD,
             )
 
@@ -87,7 +99,7 @@ def tile_picked_hash_lin_relu_sub_l_kernel(tc, xT, w, b, offs, out):
             nc.vector.quantize_mx(out=w_codes[:, m0:m1].bitcast(FP8X4), scales=w_scales[:, m0:m1], in_=src)
 
         def quantize_x(v0, v1):
-            src = x_bf[:, PACK * v0 : PACK * v1]
+            src = rounded(v0, v1)
             nc.vector.quantize_mx(out=x_codes[:, v0:v1].bitcast(FP8X4), scales=x_scales[:, v0:v1], in_=src)
 
         out_rows = out.rearrange("(j p) v -> p j v", p=P)
@@ -119,27 +131,33 @@ def tile_picked_hash_lin_relu_sub_l_kernel(tc, xT, w, b, offs, out):
         nc.scalar.activation(warm_out[:], warm_in[:], COPY)
 
         last = HALF + QUARTER
+        second = keep.tile([P, V], F32, name="second", align_bytes=64)
         for t in range(PACK):
-            spans = [(0, V)] if t < PACK - 2 else [(0, HALF), (HALF, V)]
-            for v0, v1 in spans:
-                nc.scalar.activation(plane(first, t, v0, v1), picked(t, 0, v0, v1), COPY)
+            for v0 in (0, HALF):
+                nc.scalar.activation(first_half(t, v0), picked(t, 0, v0, v0 + HALF), COPY)
             end = V if t < PACK - 1 else last
             nc.scalar.activation(plane(third, t, HALF, end), picked(t, 2, HALF, end), COPY)
+            if t == 2:
+                add_last(nc.gpsimd, 0, 2, 0, HALF)
+                nc.vector.tensor_copy(out=second[:], in_=picked(t, 1, 0, V))
+                nc.gpsimd.tensor_tensor(plane(partial, t, 0, V), late_first[0][:], second[:], ADD)
             nc.vector.tensor_copy(out=plane(third, t, 0, HALF), in_=picked(t, 2, 0, HALF))
-            for v0, v1 in spans:
-                nc.vector.tensor_tensor(plane(partial, t, v0, v1), picked(t, 1, v0, v1), plane(first, t, v0, v1), ADD)
+            if t != 2:
+                for v0 in (0, HALF):
+                    sums = plane(partial, t, v0, v0 + HALF)
+                    nc.vector.tensor_tensor(sums, picked(t, 1, v0, v0 + HALF), first_half(t, v0), ADD)
         for j in range(3):
             cast_w(j * P, (j + 1) * P)
         nc.scalar.activation(plane(third, PACK - 1, last, V), picked(PACK - 1, 2, last, V), COPY)
         cast_w(3 * P, N)
-        add_last(0, HALF)
+        add_last(nc.vector, 2, PACK, 0, HALF)
         quantize_w(0, P)
         quantize_x(0, HALF)
         quantize_w(P, 2 * P)
-        add_last(HALF, last)
+        add_last(nc.vector, 0, PACK, HALF, last)
         quantize_w(2 * P, 3 * P)
         quantize_x(HALF, last)
-        add_last(last, V)
+        add_last(nc.vector, 0, PACK, last, V)
         quantize_w(3 * P, N)
         quantize_x(last, V)
         for j in range(M_TILES):

@@ -40,13 +40,10 @@ def tile_picked_hash_lin_relu_sub_l_kernel(tc, xT, w, b, offs, out):
         for t in range(1, PACK):
             nc.sync.dma_start(out=rows[t][:], in_=x_rows[:, t, :])
         w_rows = w.rearrange("(p t) m -> p t m", t=PACK)
-        w_raw0 = keep.tile([P, PACK * N // 2], F32, name="w_raw0", align_bytes=64)
-        third_and_w = keep.tile([P, PACK * V - QUARTER + PACK * N // 2], F32, name="third_and_w", align_bytes=64)
-        third = third_and_w[:, : PACK * V]
-        w_raw = [w_raw0[:], third_and_w[:, PACK * V - QUARTER :]]
+        w_raw = [keep.tile([P, PACK * N // 2], F32, name="w_raw%d" % s, align_bytes=64) for s in range(2)]
         for s in range(2):
             cols = slice(s * N // 2, (s + 1) * N // 2)
-            nc.sync.dma_start(out=w_raw[s].rearrange("p (t m) -> p t m", t=PACK), in_=w_rows[:, :, cols])
+            nc.sync.dma_start(out=w_raw[s][:].rearrange("p (t m) -> p t m", t=PACK), in_=w_rows[:, :, cols])
         with nc.allow_non_contiguous_dma(reason="one bias value a partition"):
             nc.sync.dma_start(out=bias[:], in_=b.rearrange("(j p) o -> p (j o)", p=P))
 
@@ -55,8 +52,13 @@ def tile_picked_hash_lin_relu_sub_l_kernel(tc, xT, w, b, offs, out):
         late_first = [keep.tile([P, V], F32, name="late_first%d" % t, align_bytes=64) for t in range(2)]
         partial = keep.tile([P, PACK * V], F32, name="partial", align_bytes=64)
         w_bf = keep.tile([P, PACK * N], BF16, name="w_bf", align_bytes=64)
-        x_bf1 = keep.tile([P, PACK * HALF], BF16, name="x_bf1", align_bytes=64)
-        x_bf = [early_high[:].bitcast(BF16), x_bf1[:]]
+        third = keep.tile([P, PACK * V], F32, name="third", align_bytes=64)
+        x_bf_mid = keep.tile([P, PACK * QUARTER], BF16, name="x_bf_mid", align_bytes=64)
+        x_bf = {
+            0: early_high[:].bitcast(BF16),
+            HALF: x_bf_mid[:],
+            HALF + QUARTER: w_raw[1][:, : PACK * QUARTER // 2].bitcast(BF16),
+        }
         x_codes = keep.tile([P, V], U32, name="x_codes", align_bytes=64)
         x_scales = keep.tile([P, V], U8, name="x_scales", align_bytes=64)
         w_codes = keep.tile([P, N], U32, name="w_codes", align_bytes=64)
@@ -73,21 +75,17 @@ def tile_picked_hash_lin_relu_sub_l_kernel(tc, xT, w, b, offs, out):
                 return late_first[t - 2][:, v0 : v0 + HALF]
             return early_high[:, t * HALF : (t + 1) * HALF] if v0 else early_low[:, t, :]
 
-        def rounded(v0, v1):
-            h = v0 // HALF
-            return x_bf[h][:, PACK * (v0 - h * HALF) : PACK * (v1 - h * HALF)]
-
         def add_last(engine, t0, t1, v0, v1):
             blocks = slice(v0 // RUN, v1 // RUN)
             engine.tensor_tensor(
-                rounded(v0, v1).rearrange("p (c i t) -> p c t i", i=RUN, t=PACK)[:, :, t0:t1],
+                x_bf[v0].rearrange("p (c i t) -> p c t i", i=RUN, t=PACK)[:, :, t0:t1],
                 partial[:].rearrange("p (t c i) -> p c t i", t=PACK, i=RUN)[:, blocks, t0:t1],
-                third.rearrange("p (t c i) -> p c t i", t=PACK, i=RUN)[:, blocks, t0:t1],
+                third[:].rearrange("p (t c i) -> p c t i", t=PACK, i=RUN)[:, blocks, t0:t1],
                 ADD,
             )
 
         def cast_w(m0, m1):
-            raw = w_raw[2 * m0 // N].rearrange("p (t c i) -> p c t i", i=RUN, t=PACK)
+            raw = w_raw[2 * m0 // N][:].rearrange("p (t c i) -> p c t i", i=RUN, t=PACK)
             start = m0 % (N // 2)
             nc.scalar.copy(
                 out=w_bf[:, PACK * m0 : PACK * m1].rearrange("p (c i t) -> p c t i", i=RUN, t=PACK),
@@ -99,7 +97,7 @@ def tile_picked_hash_lin_relu_sub_l_kernel(tc, xT, w, b, offs, out):
             nc.vector.quantize_mx(out=w_codes[:, m0:m1].bitcast(FP8X4), scales=w_scales[:, m0:m1], in_=src)
 
         def quantize_x(v0, v1):
-            src = rounded(v0, v1)
+            src = x_bf[v0]
             nc.vector.quantize_mx(out=x_codes[:, v0:v1].bitcast(FP8X4), scales=x_scales[:, v0:v1], in_=src)
 
         out_rows = out.rearrange("(j p) v -> p j v", p=P)
@@ -135,8 +133,7 @@ def tile_picked_hash_lin_relu_sub_l_kernel(tc, xT, w, b, offs, out):
         for t in range(PACK):
             for v0 in (0, HALF):
                 nc.scalar.activation(first_half(t, v0), picked(t, 0, v0, v0 + HALF), COPY)
-            end = V if t < PACK - 1 else last
-            nc.scalar.activation(plane(third, t, HALF, end), picked(t, 2, HALF, end), COPY)
+            nc.scalar.activation(plane(third, t, HALF, V), picked(t, 2, HALF, V), COPY)
             if t == 2:
                 add_last(nc.gpsimd, 0, 2, 0, HALF)
                 nc.vector.tensor_copy(out=second[:], in_=picked(t, 1, 0, V))
@@ -146,10 +143,8 @@ def tile_picked_hash_lin_relu_sub_l_kernel(tc, xT, w, b, offs, out):
                 for v0 in (0, HALF):
                     sums = plane(partial, t, v0, v0 + HALF)
                     nc.vector.tensor_tensor(sums, picked(t, 1, v0, v0 + HALF), first_half(t, v0), ADD)
-        for j in range(3):
+        for j in range(M_TILES):
             cast_w(j * P, (j + 1) * P)
-        nc.scalar.activation(plane(third, PACK - 1, last, V), picked(PACK - 1, 2, last, V), COPY)
-        cast_w(3 * P, N)
         add_last(nc.vector, 2, PACK, 0, HALF)
         quantize_w(0, P)
         quantize_x(0, HALF)

@@ -20,7 +20,7 @@ P = 128
 PACK = 4
 RUN = 4
 HALF = V // 2
-QUARTER = V // 4
+EIGHTH = V // 8
 M_TILES = N // P
 
 
@@ -40,10 +40,12 @@ def tile_picked_hash_lin_relu_sub_l_kernel(tc, xT, w, b, offs, out):
         for t in range(1, PACK):
             nc.sync.dma_start(out=rows[t][:], in_=x_rows[:, t, :])
         w_rows = w.rearrange("(p t) m -> p t m", t=PACK)
-        w_raw = [keep.tile([P, PACK * N // 2], F32, name="w_raw%d" % s, align_bytes=64) for s in range(2)]
+        w_low = keep.tile([P, PACK * N // 2], F32, name="w_low", align_bytes=64)
+        w_high = keep.tile([P, 2 * HALF - P + PACK * N // 2], F32, name="w_high", align_bytes=64)
+        w_raw = [w_low[:], w_high[:, 2 * HALF - P :]]
         for s in range(2):
             cols = slice(s * N // 2, (s + 1) * N // 2)
-            nc.sync.dma_start(out=w_raw[s][:].rearrange("p (t m) -> p t m", t=PACK), in_=w_rows[:, :, cols])
+            nc.sync.dma_start(out=w_raw[s].rearrange("p (t m) -> p t m", t=PACK), in_=w_rows[:, :, cols])
         with nc.allow_non_contiguous_dma(reason="one bias value a partition"):
             nc.sync.dma_start(out=bias[:], in_=b.rearrange("(j p) o -> p (j o)", p=P))
 
@@ -51,14 +53,9 @@ def tile_picked_hash_lin_relu_sub_l_kernel(tc, xT, w, b, offs, out):
         early_high = keep.tile([P, 2 * HALF], F32, name="early_high", align_bytes=64)
         late_first = [keep.tile([P, V], F32, name="late_first%d" % t, align_bytes=64) for t in range(2)]
         partial = keep.tile([P, PACK * V], F32, name="partial", align_bytes=64)
-        w_bf = keep.tile([P, PACK * N], BF16, name="w_bf", align_bytes=64)
+        w_bf = [keep.tile([P, PACK * P], BF16, name="w_bf%d" % j, align_bytes=64) for j in range(M_TILES)]
         third = keep.tile([P, PACK * V], F32, name="third", align_bytes=64)
-        x_bf_mid = keep.tile([P, PACK * QUARTER], BF16, name="x_bf_mid", align_bytes=64)
-        x_bf = {
-            0: early_high[:].bitcast(BF16),
-            HALF: x_bf_mid[:],
-            HALF + QUARTER: w_raw[1][:, : PACK * QUARTER // 2].bitcast(BF16),
-        }
+        x_bf = [early_high[:].bitcast(BF16), w_high[:, : 2 * HALF].bitcast(BF16)]
         x_codes = keep.tile([P, V], U32, name="x_codes", align_bytes=64)
         x_scales = keep.tile([P, V], U8, name="x_scales", align_bytes=64)
         w_codes = keep.tile([P, N], U32, name="w_codes", align_bytes=64)
@@ -75,30 +72,33 @@ def tile_picked_hash_lin_relu_sub_l_kernel(tc, xT, w, b, offs, out):
                 return late_first[t - 2][:, v0 : v0 + HALF]
             return early_high[:, t * HALF : (t + 1) * HALF] if v0 else early_low[:, t, :]
 
+        def rounded(v0, v1):
+            h = v0 // HALF
+            return x_bf[h][:, PACK * (v0 - h * HALF) : PACK * (v1 - h * HALF)]
+
         def add_last(engine, t0, t1, v0, v1):
             blocks = slice(v0 // RUN, v1 // RUN)
             engine.tensor_tensor(
-                x_bf[v0].rearrange("p (c i t) -> p c t i", i=RUN, t=PACK)[:, :, t0:t1],
+                rounded(v0, v1).rearrange("p (c i t) -> p c t i", i=RUN, t=PACK)[:, :, t0:t1],
                 partial[:].rearrange("p (t c i) -> p c t i", t=PACK, i=RUN)[:, blocks, t0:t1],
                 third[:].rearrange("p (t c i) -> p c t i", t=PACK, i=RUN)[:, blocks, t0:t1],
                 ADD,
             )
 
-        def cast_w(m0, m1):
-            raw = w_raw[2 * m0 // N][:].rearrange("p (t c i) -> p c t i", i=RUN, t=PACK)
-            start = m0 % (N // 2)
+        def cast_w(j):
+            raw = w_raw[j // 2].rearrange("p (t c i) -> p c t i", i=RUN, t=PACK)
             nc.scalar.copy(
-                out=w_bf[:, PACK * m0 : PACK * m1].rearrange("p (c i t) -> p c t i", i=RUN, t=PACK),
-                in_=raw[:, start // RUN : (start + m1 - m0) // RUN],
+                out=w_bf[j][:].rearrange("p (c i t) -> p c t i", i=RUN, t=PACK),
+                in_=raw[:, j % 2 * P // RUN : (j % 2 + 1) * P // RUN],
             )
 
-        def quantize_w(m0, m1):
-            src = w_bf[:, PACK * m0 : PACK * m1]
-            nc.vector.quantize_mx(out=w_codes[:, m0:m1].bitcast(FP8X4), scales=w_scales[:, m0:m1], in_=src)
+        def quantize_w(j):
+            cols = slice(j * P, (j + 1) * P)
+            nc.vector.quantize_mx(out=w_codes[:, cols].bitcast(FP8X4), scales=w_scales[:, cols], in_=w_bf[j][:])
 
-        def quantize_x(v0, v1):
-            src = x_bf[v0]
-            nc.vector.quantize_mx(out=x_codes[:, v0:v1].bitcast(FP8X4), scales=x_scales[:, v0:v1], in_=src)
+        def quantize_x(h):
+            cols = slice(h * HALF, (h + 1) * HALF)
+            nc.vector.quantize_mx(out=x_codes[:, cols].bitcast(FP8X4), scales=x_scales[:, cols], in_=x_bf[h])
 
         out_rows = out.rearrange("(j p) v -> p j v", p=P)
         banks = [psum.tile([P, HALF], F32, name="bank%d" % n) for n in range(2 * M_TILES)]
@@ -115,20 +115,20 @@ def tile_picked_hash_lin_relu_sub_l_kernel(tc, xT, w, b, offs, out):
                 stop=True,
             )
 
-        def finish(acc, j, v0, v1, on_vector):
-            result = keep.tile([P, v1 - v0], F32, name="result%d_%d" % (v0, j))
+        results = keep.tile([P, 2 * M_TILES, HALF], F32, name="results")
+
+        def finish(acc, result, j, v0, v1, on_vector):
             if on_vector:
-                nc.vector.tensor_scalar(result[:], acc, bias[:, j : j + 1], 0.0, ADD, MAX)
+                nc.vector.tensor_scalar(result, acc, bias[:, j : j + 1], 0.0, ADD, MAX)
             else:
-                nc.scalar.activation(result[:], acc, RELU, bias=bias[:, j : j + 1])
-            nc.sync.dma_start(out=out_rows[:, j, v0:v1], in_=result[:])
+                nc.scalar.activation(result, acc, RELU, bias=bias[:, j : j + 1])
+            nc.sync.dma_start(out=out_rows[:, j, v0:v1], in_=result)
 
         warm_in = keep.tile([P, 1], F32, name="warm_in")
         warm_out = keep.tile([P, 1], F32, name="warm_out")
         nc.vector.memset(warm_in[:], 0.0)
         nc.scalar.activation(warm_out[:], warm_in[:], COPY)
 
-        last = HALF + QUARTER
         second = keep.tile([P, V], F32, name="second", align_bytes=64)
         for t in range(PACK):
             for v0 in (0, HALF):
@@ -144,22 +144,18 @@ def tile_picked_hash_lin_relu_sub_l_kernel(tc, xT, w, b, offs, out):
                     sums = plane(partial, t, v0, v0 + HALF)
                     nc.vector.tensor_tensor(sums, picked(t, 1, v0, v0 + HALF), first_half(t, v0), ADD)
         for j in range(M_TILES):
-            cast_w(j * P, (j + 1) * P)
+            cast_w(j)
         add_last(nc.vector, 2, PACK, 0, HALF)
-        quantize_w(0, P)
-        quantize_x(0, HALF)
-        quantize_w(P, 2 * P)
-        add_last(nc.vector, 0, PACK, HALF, last)
-        quantize_w(2 * P, 3 * P)
-        quantize_x(HALF, last)
-        add_last(nc.vector, 0, PACK, last, V)
-        quantize_w(3 * P, N)
-        quantize_x(last, V)
-        for j in range(M_TILES):
-            multiply(banks[j][:], j, 0, HALF)
-            finish(banks[j][:], j, 0, HALF, False)
-        for j in range(M_TILES):
-            multiply(banks[M_TILES + j][:, :QUARTER], j, HALF, last)
-        for j in range(M_TILES):
-            multiply(banks[M_TILES + j][:, QUARTER:], j, last, V)
-            finish(banks[M_TILES + j][:], j, HALF, V, j % 2 == 0)
+        quantize_w(0)
+        quantize_x(0)
+        add_last(nc.vector, 0, PACK, HALF, HALF + EIGHTH)
+        quantize_w(1)
+        quantize_w(2)
+        add_last(nc.vector, 0, PACK, HALF + EIGHTH, V)
+        quantize_w(3)
+        quantize_x(1)
+        for h in range(2):
+            for j in range(M_TILES):
+                n = h * M_TILES + j
+                multiply(banks[n][:], j, h * HALF, (h + 1) * HALF)
+                finish(banks[n][:], results[:, n, :], j, h * HALF, (h + 1) * HALF, h == 1 and j % 2 == 0)

@@ -22,6 +22,8 @@ RUN = 4
 HALF = V // 2
 EIGHTH = V // 8
 M_TILES = N // P
+QUARTER = V // 4
+OWN = 320
 
 
 def tile_picked_hash_lin_relu_sub_l_kernel(tc, xT, w, b, offs, out):
@@ -40,9 +42,9 @@ def tile_picked_hash_lin_relu_sub_l_kernel(tc, xT, w, b, offs, out):
         for t in range(1, PACK):
             nc.sync.dma_start(out=rows[t][:], in_=x_rows[:, t, :])
         w_rows = w.rearrange("(p t) m -> p t m", t=PACK)
-        w_low = keep.tile([P, PACK * N // 2], F32, name="w_low", align_bytes=64)
-        w_high = keep.tile([P, 2 * HALF - P + PACK * N // 2], F32, name="w_high", align_bytes=64)
-        w_raw = [w_low[:], w_high[:, 2 * HALF - P :]]
+        high = PACK * N // 2 + 2 * HALF - 2 * P
+        w_high = keep.tile([P, high + PACK * N // 2 + P], F32, name="w_high", align_bytes=64)
+        w_raw = [w_high[:, : PACK * N // 2], w_high[:, high : high + PACK * N // 2]]
         for s in range(2):
             cols = slice(s * N // 2, (s + 1) * N // 2)
             nc.sync.dma_start(out=w_raw[s].rearrange("p (t m) -> p t m", t=PACK), in_=w_rows[:, :, cols])
@@ -55,7 +57,7 @@ def tile_picked_hash_lin_relu_sub_l_kernel(tc, xT, w, b, offs, out):
         partial = keep.tile([P, PACK * V], F32, name="partial", align_bytes=64)
         w_bf = [keep.tile([P, PACK * P], BF16, name="w_bf%d" % j, align_bytes=64) for j in range(M_TILES)]
         third = keep.tile([P, PACK * V], F32, name="third", align_bytes=64)
-        x_bf = [early_high[:].bitcast(BF16), w_high[:, : 2 * HALF].bitcast(BF16)]
+        x_bf = [early_high[:].bitcast(BF16), w_high[:, PACK * N // 2 - P : high + P].bitcast(BF16)]
         x_codes = keep.tile([P, V], U32, name="x_codes", align_bytes=64)
         x_scales = keep.tile([P, V], U8, name="x_scales", align_bytes=64)
         w_codes = keep.tile([P, N], U32, name="w_codes", align_bytes=64)
@@ -96,9 +98,8 @@ def tile_picked_hash_lin_relu_sub_l_kernel(tc, xT, w, b, offs, out):
             cols = slice(j * P, (j + 1) * P)
             nc.vector.quantize_mx(out=w_codes[:, cols].bitcast(FP8X4), scales=w_scales[:, cols], in_=w_bf[j][:])
 
-        def quantize_x(h):
-            cols = slice(h * HALF, (h + 1) * HALF)
-            nc.vector.quantize_mx(out=x_codes[:, cols].bitcast(FP8X4), scales=x_scales[:, cols], in_=x_bf[h])
+        def quantize_x(v0, v1):
+            nc.vector.quantize_mx(out=x_codes[:, v0:v1].bitcast(FP8X4), scales=x_scales[:, v0:v1], in_=rounded(v0, v1))
 
         out_rows = out.rearrange("(j p) v -> p j v", p=P)
         banks = [psum.tile([P, HALF], F32, name="bank%d" % n) for n in range(2 * M_TILES)]
@@ -115,7 +116,9 @@ def tile_picked_hash_lin_relu_sub_l_kernel(tc, xT, w, b, offs, out):
                 stop=True,
             )
 
-        results = keep.tile([P, 2 * M_TILES, HALF], F32, name="results")
+        later = keep.tile([P, 2 * M_TILES - 2, HALF], F32, name="later")
+        results = [w_high[:, high + (3 - n) * HALF + P : high + (4 - n) * HALF + P] for n in range(2)]
+        results = results + [later[:, n, :] for n in range(2 * M_TILES - 2)]
 
         def finish(acc, result, j, v0, v1, on_vector):
             if on_vector:
@@ -130,7 +133,7 @@ def tile_picked_hash_lin_relu_sub_l_kernel(tc, xT, w, b, offs, out):
         nc.scalar.activation(warm_out[:], warm_in[:], COPY)
 
         second = keep.tile([P, V], F32, name="second", align_bytes=64)
-        for t in range(PACK):
+        for t in range(PACK - 1):
             for v0 in (0, HALF):
                 nc.scalar.activation(first_half(t, v0), picked(t, 0, v0, v0 + HALF), COPY)
             nc.scalar.activation(plane(third, t, HALF, V), picked(t, 2, HALF, V), COPY)
@@ -143,19 +146,30 @@ def tile_picked_hash_lin_relu_sub_l_kernel(tc, xT, w, b, offs, out):
                 for v0 in (0, HALF):
                     sums = plane(partial, t, v0, v0 + HALF)
                     nc.vector.tensor_tensor(sums, picked(t, 1, v0, v0 + HALF), first_half(t, v0), ADD)
+        t = PACK - 1
+        base = late_first[1]
+        nc.vector.tensor_copy(out=base[:, OWN:V], in_=picked(t, 0, OWN, V))
+        for v0, v1 in ((0, QUARTER), (QUARTER, OWN)):
+            nc.scalar.activation(base[:, v0:v1], picked(t, 0, v0, v1), COPY)
+        for v0 in (0, HALF):
+            nc.scalar.activation(plane(third, t, v0, v0 + HALF), picked(t, 2, v0, v0 + HALF), COPY)
+        for v0, v1 in ((0, QUARTER), (QUARTER, HALF), (HALF, V)):
+            nc.vector.tensor_tensor(plane(partial, t, v0, v1), picked(t, 1, v0, v1), base[:, v0:v1], ADD)
         for j in range(M_TILES):
             cast_w(j)
         add_last(nc.vector, 2, PACK, 0, HALF)
         quantize_w(0)
-        quantize_x(0)
-        add_last(nc.vector, 0, PACK, HALF, HALF + EIGHTH)
+        quantize_x(0, HALF)
+        add_last(nc.vector, 0, PACK, HALF + QUARTER, V - EIGHTH)
         quantize_w(1)
+        add_last(nc.vector, 0, PACK, HALF, HALF + QUARTER)
         quantize_w(2)
-        add_last(nc.vector, 0, PACK, HALF + EIGHTH, V)
+        add_last(nc.vector, 0, PACK, V - EIGHTH, V)
         quantize_w(3)
-        quantize_x(1)
+        quantize_x(HALF, HALF + QUARTER)
+        quantize_x(HALF + QUARTER, V)
         for h in range(2):
             for j in range(M_TILES):
                 n = h * M_TILES + j
                 multiply(banks[n][:], j, h * HALF, (h + 1) * HALF)
-                finish(banks[n][:], results[:, n, :], j, h * HALF, (h + 1) * HALF, h == 1 and j % 2 == 0)
+                finish(banks[n][:], results[n], j, h * HALF, (h + 1) * HALF, n >= M_TILES - 1 and j % 2 == 1)

@@ -23,7 +23,6 @@ HALF = V // 2
 EIGHTH = V // 8
 M_TILES = N // P
 QUARTER = V // 4
-OWN = 320
 
 
 def tile_picked_hash_lin_relu_sub_l_kernel(tc, xT, w, b, offs, out):
@@ -148,11 +147,11 @@ def tile_picked_hash_lin_relu_sub_l_kernel(tc, xT, w, b, offs, out):
                     nc.vector.tensor_tensor(sums, picked(t, 1, v0, v0 + HALF), first_half(t, v0), ADD)
         t = PACK - 1
         base = late_first[1]
-        nc.vector.tensor_copy(out=base[:, OWN:V], in_=picked(t, 0, OWN, V))
-        for v0, v1 in ((0, QUARTER), (QUARTER, OWN)):
-            nc.scalar.activation(base[:, v0:v1], picked(t, 0, v0, v1), COPY)
+        nc.scalar.activation(base[:, HALF:V], picked(t, 0, HALF, V), COPY)
         for v0 in (0, HALF):
             nc.scalar.activation(plane(third, t, v0, v0 + HALF), picked(t, 2, v0, v0 + HALF), COPY)
+        for v0 in (0, QUARTER):
+            nc.vector.tensor_copy(out=base[:, v0 : v0 + QUARTER], in_=picked(t, 0, v0, v0 + QUARTER))
         for v0, v1 in ((0, QUARTER), (QUARTER, HALF), (HALF, V)):
             nc.vector.tensor_tensor(plane(partial, t, v0, v1), picked(t, 1, v0, v1), base[:, v0:v1], ADD)
         for j in range(M_TILES):

@@ -132,28 +132,27 @@ def tile_picked_hash_lin_relu_sub_l_kernel(tc, xT, w, b, offs, out):
         nc.scalar.activation(warm_out[:], warm_in[:], COPY)
 
         second = keep.tile([P, V], F32, name="second", align_bytes=64)
-        for t in range(PACK - 1):
-            for v0 in (0, HALF):
-                nc.scalar.activation(first_half(t, v0), picked(t, 0, v0, v0 + HALF), COPY)
-            nc.scalar.activation(plane(third, t, HALF, V), picked(t, 2, HALF, V), COPY)
+        for t in range(PACK):
             if t == 2:
-                add_last(nc.gpsimd, 0, 2, 0, HALF)
-                nc.vector.tensor_copy(out=second[:], in_=picked(t, 1, 0, V))
-                nc.gpsimd.tensor_tensor(plane(partial, t, 0, V), late_first[0][:], second[:], ADD)
-            nc.vector.tensor_copy(out=plane(third, t, 0, HALF), in_=picked(t, 2, 0, HALF))
-            if t != 2:
                 for v0 in (0, HALF):
-                    sums = plane(partial, t, v0, v0 + HALF)
-                    nc.vector.tensor_tensor(sums, picked(t, 1, v0, v0 + HALF), first_half(t, v0), ADD)
-        t = PACK - 1
-        base = late_first[1]
-        nc.scalar.activation(base[:, HALF:V], picked(t, 0, HALF, V), COPY)
-        for v0 in (0, HALF):
-            nc.scalar.activation(plane(third, t, v0, v0 + HALF), picked(t, 2, v0, v0 + HALF), COPY)
-        for v0 in (0, QUARTER):
-            nc.vector.tensor_copy(out=base[:, v0 : v0 + QUARTER], in_=picked(t, 0, v0, v0 + QUARTER))
-        for v0, v1 in ((0, QUARTER), (QUARTER, HALF), (HALF, V)):
-            nc.vector.tensor_tensor(plane(partial, t, v0, v1), picked(t, 1, v0, v1), base[:, v0:v1], ADD)
+                    nc.scalar.activation(first_half(t, v0), picked(t, 0, v0, v0 + HALF), COPY)
+                nc.scalar.activation(plane(third, t, HALF, V), picked(t, 2, HALF, V), COPY)
+                add_last(nc.gpsimd, 0, 2, 0, HALF)
+                for v0 in (0, HALF):
+                    ids = slice(v0, v0 + HALF)
+                    nc.vector.tensor_copy(out=second[:, ids], in_=picked(t, 1, v0, v0 + HALF))
+                    nc.gpsimd.tensor_tensor(plane(partial, t, v0, v0 + HALF), first_half(t, v0), second[:, ids], ADD)
+                nc.vector.tensor_copy(out=plane(third, t, 0, HALF), in_=picked(t, 2, 0, HALF))
+                continue
+            nc.scalar.activation(first_half(t, HALF), picked(t, 0, HALF, V), COPY)
+            for v0 in (0, HALF):
+                nc.scalar.activation(plane(third, t, v0, v0 + HALF), picked(t, 2, v0, v0 + HALF), COPY)
+            for v0 in (0, QUARTER):
+                nc.vector.tensor_copy(out=first_half(t, 0)[:, v0 : v0 + QUARTER], in_=picked(t, 0, v0, v0 + QUARTER))
+            for v0 in (0, QUARTER):
+                own = first_half(t, 0)[:, v0 : v0 + QUARTER]
+                nc.vector.tensor_tensor(plane(partial, t, v0, v0 + QUARTER), picked(t, 1, v0, v0 + QUARTER), own, ADD)
+            nc.vector.tensor_tensor(plane(partial, t, HALF, V), picked(t, 1, HALF, V), first_half(t, HALF), ADD)
         for j in range(M_TILES):
             cast_w(j)
         add_last(nc.vector, 2, PACK, 0, HALF)

@@ -1,6 +1,7 @@
 from contextlib import ExitStack
 
 import concourse.mybir as mybir
+from concourse.masks import make_identity
 
 K, T, D, V, N = 512, 2048, 3, 512, 512
 FLOPS = 2 * K * N * V
@@ -40,6 +41,9 @@ def tile_picked_hash_lin_relu_sub_l_kernel(tc, xT, w, b, offs, out):
         nc.sync.dma_start(offsets[:], offs)
         for t in range(1, PACK):
             nc.sync.dma_start(out=rows[t][:], in_=x_rows[:, t, :])
+        bias_rows = keep.tile([P, P], F32, name="bias_rows")
+        nc.vector.memset(bias_rows[:], 0.0)
+        nc.sync.dma_start(out=bias_rows[:M_TILES, :], in_=b.rearrange("(j p) o -> j (p o)", p=P))
         w_rows = w.rearrange("(p t) m -> p t m", t=PACK)
         high = PACK * N // 2 + 2 * HALF - 2 * P
         w_high = keep.tile([P, high + PACK * N // 2 + P], F32, name="w_high", align_bytes=64)
@@ -47,8 +51,6 @@ def tile_picked_hash_lin_relu_sub_l_kernel(tc, xT, w, b, offs, out):
         for s in range(2):
             cols = slice(s * N // 2, (s + 1) * N // 2)
             nc.sync.dma_start(out=w_raw[s].rearrange("p (t m) -> p t m", t=PACK), in_=w_rows[:, :, cols])
-        with nc.allow_non_contiguous_dma(reason="one bias value a partition"):
-            nc.sync.dma_start(out=bias[:], in_=b.rearrange("(j p) o -> p (j o)", p=P))
 
         early_low = keep.tile([P, 2, HALF], F32, name="early_low", align_bytes=64)
         early_high = keep.tile([P, 2 * HALF], F32, name="early_high", align_bytes=64)
@@ -126,6 +128,11 @@ def tile_picked_hash_lin_relu_sub_l_kernel(tc, xT, w, b, offs, out):
                 nc.scalar.activation(result, acc, RELU, bias=bias[:, j : j + 1])
             nc.sync.dma_start(out=out_rows[:, j, v0:v1], in_=result)
 
+        identity = keep.tile([P, P], F32, name="identity")
+        make_identity(nc, identity[:])
+        turned = banks[2 * M_TILES - 1][:, :P]
+        nc.tensor.transpose(turned, bias_rows[:], identity[:])
+
         warm_in = keep.tile([P, 1], F32, name="warm_in")
         warm_out = keep.tile([P, 1], F32, name="warm_out")
         nc.vector.memset(warm_in[:], 0.0)
@@ -153,6 +160,7 @@ def tile_picked_hash_lin_relu_sub_l_kernel(tc, xT, w, b, offs, out):
                 own = first_half(t, 0)[:, v0 : v0 + QUARTER]
                 nc.vector.tensor_tensor(plane(partial, t, v0, v0 + QUARTER), picked(t, 1, v0, v0 + QUARTER), own, ADD)
             nc.vector.tensor_tensor(plane(partial, t, HALF, V), picked(t, 1, HALF, V), first_half(t, HALF), ADD)
+        nc.scalar.copy(out=bias[:], in_=turned[:, :M_TILES])
         for j in range(M_TILES):
             cast_w(j)
         add_last(nc.vector, 2, PACK, 0, HALF)

from contextlib import ExitStack

import concourse.mybir as mybir
from concourse.masks import make_identity

K, T, D, V, N = 512, 2048, 3, 512, 512
FLOPS = 2 * K * N * V

F32 = mybir.dt.float32
BF16 = mybir.dt.bfloat16
U32 = mybir.dt.uint32
U16 = mybir.dt.uint16
U8 = mybir.dt.uint8
FP8X4 = mybir.dt.float8_e4m3fn_x4
ADD = mybir.AluOpType.add
MAX = mybir.AluOpType.max
RELU = mybir.ActivationFunctionType.Relu
COPY = mybir.ActivationFunctionType.Copy

P = 128
PACK = 4
RUN = 4
HALF = V // 2
EIGHTH = V // 8
M_TILES = N // P
QUARTER = V // 4


def tile_picked_hash_lin_relu_sub_l_kernel(tc, xT, w, b, offs, out):
    nc = tc.nc
    with ExitStack() as ctx:
        keep = ctx.enter_context(tc.tile_pool(name="keep", bufs=1))
        psum = ctx.enter_context(tc.psum_pool(name="psum", bufs=1))

        offsets = keep.tile([P, D * V // 16], U16, name="offsets")
        bias = keep.tile([P, M_TILES], F32, name="bias")

        x_rows = xT.rearrange("(p t) c -> p t c", t=PACK)
        rows = [keep.tile([P, T], F32, name="row%d" % t) for t in range(PACK)]
        nc.sync.dma_start(out=rows[0][:], in_=x_rows[:, 0, :])
        nc.sync.dma_start(offsets[:], offs)
        for t in range(1, PACK):
            nc.sync.dma_start(out=rows[t][:], in_=x_rows[:, t, :])
        bias_rows = keep.tile([P, P], F32, name="bias_rows")
        nc.vector.memset(bias_rows[:], 0.0)
        nc.sync.dma_start(out=bias_rows[:M_TILES, :], in_=b.rearrange("(j p) o -> j (p o)", p=P))
        w_rows = w.rearrange("(p t) m -> p t m", t=PACK)
        high = PACK * N // 2 + 2 * HALF - 2 * P
        w_high = keep.tile([P, high + PACK * N // 2 + P], F32, name="w_high", align_bytes=64)
        w_raw = [w_high[:, : PACK * N // 2], w_high[:, high : high + PACK * N // 2]]
        for s in range(2):
            cols = slice(s * N // 2, (s + 1) * N // 2)
            nc.sync.dma_start(out=w_raw[s].rearrange("p (t m) -> p t m", t=PACK), in_=w_rows[:, :, cols])

        early_low = keep.tile([P, 2, HALF], F32, name="early_low", align_bytes=64)
        early_high = keep.tile([P, 2 * HALF], F32, name="early_high", align_bytes=64)
        late_first = [keep.tile([P, V], F32, name="late_first%d" % t, align_bytes=64) for t in range(2)]
        partial = keep.tile([P, PACK * V], F32, name="partial", align_bytes=64)
        w_bf = [keep.tile([P, PACK * P], BF16, name="w_bf%d" % j, align_bytes=64) for j in range(M_TILES)]
        third = keep.tile([P, PACK * V], F32, name="third", align_bytes=64)
        x_bf = [early_high[:].bitcast(BF16), w_high[:, PACK * N // 2 - P : high + P].bitcast(BF16)]
        x_codes = keep.tile([P, V], U32, name="x_codes", align_bytes=64)
        x_scales = keep.tile([P, V], U8, name="x_scales", align_bytes=64)
        w_codes = keep.tile([P, N], U32, name="w_codes", align_bytes=64)
        w_scales = keep.tile([P, N], U8, name="w_scales", align_bytes=64)

        def picked(t, d, v0, v1):
            return rows[t][:].indirect(offsets[:, (d * V + v0) // 16 : (d * V + v1) // 16])

        def plane(tile, t, v0, v1):
            return tile[:, t * V + v0 : t * V + v1]

        def first_half(t, v0):
            if t >= 2:
                return late_first[t - 2][:, v0 : v0 + HALF]
            return early_high[:, t * HALF : (t + 1) * HALF] if v0 else early_low[:, t, :]

        def rounded(v0, v1):
            h = v0 // HALF
            return x_bf[h][:, PACK * (v0 - h * HALF) : PACK * (v1 - h * HALF)]

        def add_last(engine, t0, t1, v0, v1):
            blocks = slice(v0 // RUN, v1 // RUN)
            engine.tensor_tensor(
                rounded(v0, v1).rearrange("p (c i t) -> p c t i", i=RUN, t=PACK)[:, :, t0:t1],
                partial[:].rearrange("p (t c i) -> p c t i", t=PACK, i=RUN)[:, blocks, t0:t1],
                third[:].rearrange("p (t c i) -> p c t i", t=PACK, i=RUN)[:, blocks, t0:t1],
                ADD,
            )

        def cast_w(j):
            raw = w_raw[j // 2].rearrange("p (t c i) -> p c t i", i=RUN, t=PACK)
            nc.scalar.copy(
                out=w_bf[j][:].rearrange("p (c i t) -> p c t i", i=RUN, t=PACK),
                in_=raw[:, j % 2 * P // RUN : (j % 2 + 1) * P // RUN],
            )

        def quantize_w(j):
            cols = slice(j * P, (j + 1) * P)
            nc.vector.quantize_mx(out=w_codes[:, cols].bitcast(FP8X4), scales=w_scales[:, cols], in_=w_bf[j][:])

        def quantize_x(v0, v1):
            nc.vector.quantize_mx(out=x_codes[:, v0:v1].bitcast(FP8X4), scales=x_scales[:, v0:v1], in_=rounded(v0, v1))

        out_rows = out.rearrange("(j p) v -> p j v", p=P)
        banks = [psum.tile([P, HALF], F32, name="bank%d" % n) for n in range(2 * M_TILES)]

        def multiply(acc, j, v0, v1):
            m_cols = slice(j * P, (j + 1) * P)
            nc.tensor.matmul_mx(
                out=acc,
                lhsT=w_codes[:, m_cols].bitcast(FP8X4),
                lhsT_scale=w_scales[:, m_cols],
                rhs=x_codes[:, v0:v1].bitcast(FP8X4),
                rhs_scale=x_scales[:, v0:v1],
                start=True,
                stop=True,
            )

        later = keep.tile([P, 2 * M_TILES - 2, HALF], F32, name="later")
        results = [w_high[:, high + (3 - n) * HALF + P : high + (4 - n) * HALF + P] for n in range(2)]
        results = results + [later[:, n, :] for n in range(2 * M_TILES - 2)]

        def finish(acc, result, j, v0, v1, on_vector):
            if on_vector:
                nc.vector.tensor_scalar(result, acc, bias[:, j : j + 1], 0.0, ADD, MAX)
            else:
                nc.scalar.activation(result, acc, RELU, bias=bias[:, j : j + 1])
            nc.sync.dma_start(out=out_rows[:, j, v0:v1], in_=result)

        identity = keep.tile([P, P], F32, name="identity")
        make_identity(nc, identity[:])
        turned = banks[2 * M_TILES - 1][:, :P]
        nc.tensor.transpose(turned, bias_rows[:], identity[:])

        warm_in = keep.tile([P, 1], F32, name="warm_in")
        warm_out = keep.tile([P, 1], F32, name="warm_out")
        nc.vector.memset(warm_in[:], 0.0)
        nc.scalar.activation(warm_out[:], warm_in[:], COPY)

        second = keep.tile([P, V], F32, name="second", align_bytes=64)
        for t in range(PACK):
            if t == 2:
                for v0 in (0, HALF):
                    nc.scalar.activation(first_half(t, v0), picked(t, 0, v0, v0 + HALF), COPY)
                nc.scalar.activation(plane(third, t, HALF, V), picked(t, 2, HALF, V), COPY)
                add_last(nc.gpsimd, 0, 2, 0, HALF)
                for v0 in (0, HALF):
                    ids = slice(v0, v0 + HALF)
                    nc.vector.tensor_copy(out=second[:, ids], in_=picked(t, 1, v0, v0 + HALF))
                    nc.gpsimd.tensor_tensor(plane(partial, t, v0, v0 + HALF), first_half(t, v0), second[:, ids], ADD)
                nc.vector.tensor_copy(out=plane(third, t, 0, HALF), in_=picked(t, 2, 0, HALF))
                continue
            nc.scalar.activation(first_half(t, HALF), picked(t, 0, HALF, V), COPY)
            for v0 in (0, HALF):
                nc.scalar.activation(plane(third, t, v0, v0 + HALF), picked(t, 2, v0, v0 + HALF), COPY)
            for v0 in (0, QUARTER):
                nc.vector.tensor_copy(out=first_half(t, 0)[:, v0 : v0 + QUARTER], in_=picked(t, 0, v0, v0 + QUARTER))
            for v0 in (0, QUARTER):
                own = first_half(t, 0)[:, v0 : v0 + QUARTER]
                nc.vector.tensor_tensor(plane(partial, t, v0, v0 + QUARTER), picked(t, 1, v0, v0 + QUARTER), own, ADD)
            nc.vector.tensor_tensor(plane(partial, t, HALF, V), picked(t, 1, HALF, V), first_half(t, HALF), ADD)
        nc.scalar.copy(out=bias[:], in_=turned[:, :M_TILES])
        for j in range(M_TILES):
            cast_w(j)
        add_last(nc.vector, 2, PACK, 0, HALF)
        quantize_w(0)
        quantize_x(0, HALF)
        add_last(nc.vector, 0, PACK, HALF + QUARTER, V - EIGHTH)
        quantize_w(1)
        add_last(nc.vector, 0, PACK, HALF, HALF + QUARTER)
        quantize_w(2)
        add_last(nc.vector, 0, PACK, V - EIGHTH, V)
        quantize_w(3)
        quantize_x(HALF, HALF + QUARTER)
        quantize_x(HALF + QUARTER, V)
        for h in range(2):
            for j in range(M_TILES):
                n = h * M_TILES + j
                multiply(banks[n][:], j, h * HALF, (h + 1) * HALF)
                finish(banks[n][:], results[n], j, h * HALF, (h + 1) * HALF, n >= M_TILES - 1 and j % 2 == 1)
